import numpy as np, ml_dtypes
CORES = [1,5,17,21,33,37,49,53]
N = 8
BF = ml_dtypes.bfloat16
def gentries(a):
    return np.ascontiguousarray(a.reshape(8, 16, -1).transpose(0, 2, 1)).reshape(8, -1)
def gtable(e):
    e = np.asarray(e); return np.ascontiguousarray(e.reshape(8, -1, 16).transpose(0, 2, 1)).reshape(128, -1).astype(np.int32)
L, T, K, R = 384, 8, 8, 4
W = L * T
def mix(rng, a):
    return np.take_along_axis(a, np.argsort(rng.random(a.shape), axis=2), 2)
def spots(rng, q, m, n):
    a = np.add.accumulate(rng.integers(1, n // m + 1, (q, 8, m, L)), axis=2)
    return mix(rng, (a + rng.integers(0, n, (q, 8, 1, L))) % n)
def reals(rng, n):
    v = 2 * rng.random((N, 8, 16, n)) - 1
    return np.where(v < 0, -1.0, 1.0) * (0.25 + 0.75 * np.abs(v)) * rng.choice(np.array([0.5, 0.75, 1.0]), (N, 8, 1, n))
def parts(rng):
    pa = rng.integers(-128, 128, (N, 8, 16, W)); fc = rng.integers(-128, 128, (N, 8, 16, R * L))
    return pa, reals(rng, W), spots(rng, N, K, W), fc, reals(rng, R * L), np.exp2(-5 + 3 * rng.random((N, 8, 16, 1)))
def flat(a):
    return np.asarray(a, np.float32).reshape(N, 128, -1).astype(BF)
def pack(pa, ea, nd, fc, er, dl):
    return {"pa": flat(pa), "ea": flat(ea), "nd": np.stack([gtable(a.reshape(8, K * L)) for a in nd]), "fc": flat(fc), "er": flat(er),
            "dl": np.clip(np.asarray(dl, np.float32), np.float32(0.03125), np.float32(0.25)).reshape(N, 128, 1)}
def setup_inputs(rng):
    return pack(*parts(rng))
def setup_inputs_spread(rng):
    pa, ea, nd, fc, er, dl = parts(rng)
    pa = np.floor((2 * rng.random(pa.shape) - 1) * np.exp2(rng.integers(3, 8, (N, 8, 1, W))))
    fc = np.floor((2 * rng.random(fc.shape) - 1) * np.exp2(rng.integers(3, 8, (N, 8, 1, R * L))))
    ea = ea * np.exp2(-rng.integers(0, 2, (N, 8, 1, W)))
    er = er * np.exp2(-rng.integers(0, 2, (N, 8, 1, R * L)))
    return pack(pa, ea, nd, fc, er, dl)
def setup_inputs_ends(rng):
    pa, ea, nd, fc, er, dl = parts(rng)
    def ends(n):
        whole = rng.random((N, 8, 1, n)) < 0.5
        return np.where(whole, rng.random((N, 8, 1, n)) < 0.5, rng.random((N, 8, 16, n)) < 0.5)
    pa = np.where(ends(W), 127, -128); fc = np.where(ends(R * L), 127, -128)
    pa[..., [1, W - 2, W - 1]] = 127; pa[..., [2, W - 3]] = -128
    for t in range(R): fc[..., t * L + L - 1] = 127 if t % 2 else -128
    ea = np.where(ends(W), 1.0, -1.0); er = np.where(ends(R * L), 1.0, -1.0); dl = np.where(rng.random(dl.shape) < 0.5, 0.25, 0.03125)
    ea[:, :, 0] = 1.0; er[:, :, 0] = -1.0; ea[:, :, 15] = -1.0; er[:, :, 15] = 1.0
    dl[:, :, 0] = 0.25; dl[:, :, 15] = 0.25; dl[:, :, 1] = 0.03125
    a = rng.integers(1, K, (N, 8, 1, L)); a[N - 1, :, 0, L - 1] = K // 2; j = np.arange(K)[:, None]
    far = np.where(j < a, j, W - K + j)
    near = T * (1 + spots(rng, N, K, L - 2)) + rng.choice(np.array([0, T - 2, T - 1]), (N, 8, K, L)); near[:, :, 0] = 0; near[:, :, 1] = W - 1
    nd = np.where((np.arange(8) % 2 == 1)[None, :, None, None], far, near)
    return pack(pa, ea, mix(rng, nd), fc, er, dl)
def setup_inputs_corners(rng):
    pa, ea, nd, fc, er, dl = parts(rng); one = spots(rng, 1, N * K, W)[0]; s = spots(rng, N, K, L); j = np.arange(K)[:, None]; i = np.arange(L)
    for q in range(N):
        nd[q, 0] = one[0, :K]
        nd[q, 1] = np.concatenate([one[1, :K - 1], one[1, K - 1 + q:K + q]])
        nd[q, 2] = one[2, q * K:(q + 1) * K]
        nd[q, 6] = np.where(j < (i % (K + 1))[None, :], one[6, :K], one[6, q * K:(q + 1) * K])
    nd[:, 3] = s[:, 3] * T + T - 1
    nd[:, 4] = (T * rng.integers(0, L, (N, 1, L)) + j) % W
    nd[:, 5] = ((s[:, 5] - s[:, 5, :1] + i) % L) * T + rng.choice(np.array([0, T - 2, T - 1]), (N, K, L))
    pa[::2, 7] = -128; pa[1::2, 7] = np.where(rng.random((N // 2, 1, W)) < 0.5, 127, -128)
    dl[:, ::2, ::2] = 0.03125; dl[:, 1::2, ::4] = 0.25
    return pack(pa, ea, mix(rng, nd), fc, er, dl)
def setup_inputs_crowd(rng):
    pa, ea, nd, fc, er, dl = parts(rng)
    pa[:, ::2] = rng.integers(-1, 2, (N, 4, 1, W)); fc[:, ::2] = rng.integers(-1, 2, (N, 4, 1, R * L))
    s = spots(rng, N, K, L)[..., :1]; day = np.where(np.arange(K)[:, None] % 2 == 0, T - 2, rng.integers(0, T, (N, 8, K, 1)))
    c = s * T + day; c[:, 0] = c[:1, 0]
    same = np.zeros((N, 8, K, L), np.int64) + c
    same[:, 4:, :, L - 1] = nd[:, 4:, :, L - 1]
    nd = mix(rng, same); nd[:, 1] = same[:, 1]
    return pack(pa, ea, nd, fc, er, dl)
def setup_inputs_late(rng):
    pa, ea, nd, fc, er, dl = parts(rng); c = spots(rng, N, K, L); i = np.arange(L)
    def off(n, few):
        if few: return (np.arange(16)[:, None] == rng.integers(0, 32, (N, 1, n))).astype(np.int64)
        return rng.integers(0, 8, (N, 16, n))
    for g, few in ((1, False), (3, True), (4, False), (7, True)):
        a = off(W, few); w = off(R * L, few); low = (np.arange(R * L) // L + g) % 2 == 1
        pa[:, g] = 127 - a if g % 2 else a - 128
        fc[:, g] = np.where(low, w - 128, 127 - w)
    s = spots(rng, N, K, L // 2)[:, 6]
    c[:, 6] = 2 * s + (i + (np.arange(K)[:, None] == K - 1)) % 2
    x = rng.choice(np.array([-1.0, 1.0]), (N, 16, 1)) * np.where((np.arange(R)[:, None] + i) % 2 == 0, 1.0, -1.0).reshape(-1)
    er[:, 6] = x; ea[:, 6, :, T - 1::T] = -x[:, :, :L]; dl[:, 6] = 0.25
    return pack(pa, ea, mix(rng, c * T + T - 2), fc, er, dl)
def check_ranges(d):
    bad = []
    for k, lo, hi in (("pa", -128, 127), ("fc", -128, 127), ("ea", -1, 1), ("er", -1, 1), ("dl", 0.03125, 0.25), ("nd", 0, W - 1)):
        v = np.asarray(d[k]).astype(np.float64)
        if not (np.min(v) >= lo and np.max(v) <= hi): bad.append("range of " + k)
        elif k in ("pa", "fc") and np.any(v != np.floor(v)): bad.append(k + " holds a number that isn't whole")
        elif k in ("ea", "er") and np.any(np.abs(v) < 0.0625): bad.append("sizes of " + k)
    s = np.sort(np.stack([gentries(a) for a in d["nd"]]).reshape(N, 8, K, L), axis=2)
    if np.any(s[:, :, 1:] == s[:, :, :-1]): bad.append("nd names a place twice in one lane")
    return bad
def reference(pa, ea, nd, fc, er, dl):
    P = pa.astype(np.int32).reshape(N, 8, 16, W); E = ea.astype(np.float64).reshape(N, 8, 16, W)
    f = fc.astype(np.int32).reshape(N, 8, 16, R, L); z = er.astype(np.float64).reshape(N, 8, 16, R, L); lim = dl.astype(np.float64).reshape(N, 8, 16, 1)
    A = np.stack([gentries(a) for a in nd]).astype(np.int64).reshape(N, 8, K, L)
    yb, ys = [], []
    for t in range(R):
        own = A - A % T + (A + 1) % T
        come = np.roll(own, 1, axis=0)
        void = np.any(come[:, :, :, None, :] == own[:, :, None, :, :], axis=3)
        c = np.concatenate([own, come], axis=2)
        g = np.take_along_axis(P, c.reshape(N, 8, 1, 2 * K * L), 3).reshape(N, 8, 16, 2 * K, L)
        d = np.add.reduce(np.abs(g - f[:, :, :, t][:, :, :, None, :]), axis=2)
        d[:, :, K:] = np.where(void, 2 ** 20, d[:, :, K:])
        o = np.argsort(d, axis=2, kind="stable")[:, :, :K][:, :, ::-1]
        A = np.take_along_axis(c, o, 2)
        e = np.take_along_axis(E, A.reshape(N, 8, 1, K * L), 3).reshape(N, 8, 16, K, L)
        b = np.zeros((N, 8, 16, L))
        for k in range(K): b = b + np.minimum(np.maximum(0.5 * (e[:, :, :, k] - b), -lim), lim)
        yb.append(b); ys.append(np.add.reduce(np.exp(-np.abs(e - b[:, :, :, None, :])), axis=3))
        if t < R - 1:
            P[..., t::T] = f[:, :, :, t]; E[..., t::T] = z[:, :, :, t] - b
    return {"yb": np.concatenate(yb, axis=3).reshape(N, 128, R * L).astype(np.float32), "ys": np.concatenate(ys, axis=3).reshape(N, 128, R * L).astype(np.float32)}

def check_inputs(d):
    bad = list(check_ranges(d))
    if not bad:
        for name, y in reference(**d).items():
            for q in range(N):
                v = np.abs(np.asarray(y[q], np.float64)); s = np.sqrt(np.mean(v * v))
                if v.max() > 9 * s or s < 2.0 ** -4: bad.append('%s of rank %d is uneven or too small' % (name, q))
    return bad

@@ -1,0 +1,547 @@
+import numpy as np
+from concourse.mybir import AluOpType as ALU, ActivationFunctionType as ACT
+
+L, K, R, W, C = 384, 8, 4, 3072, 24
+
+CFG = {
+    "H": 1,
+    "split": [True] * 4,
+    "halves": [2, 2, 2, 2],
+}
+CFG.update({'H': 1, 'split': [True, True, True, True], 'vabs': 2, 'chain': ['Q', 'P', 'P', 'P'], 'bias': {'s30': 2, 'o00': 58, 'e20': -5, 'g00': 1, 's00': 32, 'a00': 22, 'p0': -53, 'o30': 43, 'o10': 78, 'p3': -26, 'g10': -32, 'p2': -28, 's10': -13, 'e30': 102, 'p1': -34, 'a10': 38, 'o20': 46, 'a20': 25, 's20': -20, 'e10': -14, 'g20': 41, 'e00': 17, 'g30': -31, 'a30': -5}, 'pieces': [[[(0, 4, 'S'), (4, 8, 'V'), (8, 11, 'V'), (11, 14, 'B'), (14, 16, 'B')]], [[(0, 3, 'V'), (3, 5, 'S'), (5, 8, 'B'), (8, 10, 'B'), (10, 13, 'S'), (13, 16, 'V')]], [[(0, 2, 'S'), (2, 5, 'V'), (5, 8, 'B'), (8, 12, 'B'), (12, 14, 'S'), (14, 16, 'V')]], [[(0, 3, 'V'), (3, 6, 'S'), (6, 8, 'B'), (8, 11, 'B'), (11, 13, 'B'), (13, 16, 'B')]]], 'halves': [2, 2, 2, 2], 'egather': ['SVSS', 'SSSS', 'SSVS', 'VSVS'], 'look': 0})
+
+
+def scratch(H):
+    ch, lh = C // H, L // H
+    s = {
+        "ndl": ("sbuf", [128, K, C], "int32"), "tmpi": ("sbuf", [128, K, C], "int32"),
+        "pw": ("sbuf", [128, W], "bfloat16"), "eraw": ("sbuf", [128, W], "bfloat16"), "ew": ("sbuf", [128, W], "float32"),
+        "fr": ("sbuf", [128, R * H, 4 * L], "bfloat16"), "xr": ("sbuf", [128, R * L], "bfloat16"),
+        "dls": ("sbuf", [128, 1], "float32"), "mc": ("sbuf", [128, 16], "float32"),
+        "uu": ("sbuf", [128, L], "float32"), "r1": ("sbuf", [128, L], "float32"), "so": ("sbuf", [128, L], "float32"),
+        "wm": ("sbuf", [128, 144], "bfloat16"), "wt": ("sbuf", [128, 8], "bfloat16"),
+        "onesf": ("sbuf", [128, 128], "float32"), "idf": ("sbuf", [128, 128], "float32"), "hf": ("sbuf", [128, 128], "float32"),
+        "idb": ("sbuf", [128, 128], "bfloat16"), "big": ("sbuf", [128, 128], "bfloat16"),
+        "t1": ("sbuf", [128, 192], "bfloat16"), "t2": ("sbuf", [128, 16 * ch], "bfloat16"), "t3": ("sbuf", [128, 192], "bfloat16"),
+    }
+    for t in range(R):
+        s["ga%d" % t] = ("sbuf", [128, H, K * lh], "float32")
+        s["bs%d" % t] = ("sbuf", [128, H, (4 if t < R - 1 else 1) * lh], "float32")
+    for h in range(H):
+        s["off%d" % h] = ("sbuf", [128, 5 * 16 * ch], "uint16")
+        for t in range(R + 1):
+            s["msg%d%d" % (t, h)] = ("sbuf", [128, 2, 3, K, ch], "int32")
+        s["dd%d" % h] = ("sbuf", [128, 16 * lh], "bfloat16")
+        s["rr%d" % h] = ("sbuf", [128, 16 * lh], "bfloat16")
+        s["eq%d" % h] = ("sbuf", [128, K, K * ch], "bfloat16")
+        s["ss%d" % h] = ("sbuf", [128, 2, 17, 2 * ch], "float32")
+        s["fin%d" % h] = ("sbuf", [128, K, 2 * ch], "int32")
+    for h in range(H):
+        s["kp%d" % h] = ("psum", [128, 2, K, 64 // H], "float32")
+    for b in ("xp", "bp0", "bp1", "bp2"):
+        s[b] = ("psum", [128, 512], "float32")
+    s["sp"] = ("psum", [128, 2 * H, 10, 2 * ch], "float32")
+    return s
+
+
+SCRATCH = scratch(CFG["H"])
+SEMAPHORES = ["cV", "cS", "cP", "cG"] + ["d%d" % i for i in range(140)]
+
+CY, PE, GA, HOP = 1.04, 0.52, 1.56, 80.0
+ALL = slice(None)
+PLAN = {}
+NET8 = [
+    (0, ("S", [4, 6]), [0, 2], [0, 2]), (1, ("S", [5, 7]), [0, 2], [0, 2]),
+    (0, ("P", [4, 6]), [1, 3], [1, 3]), (1, ("P", [5, 7]), [1, 3], [1, 3]),
+    (0, ("S", [8, 12]), [4, 5], [4, 5]), (1, ("P", [0, 8]), [4, 5], [4, 5]),
+    (0, ("P", [2, 3]), [6, 7], [6, 7]), (1, ("S", [0, 11]), [6, 7], [6, 7]),
+    (0, ("S", [9]), [12], [0]), (1, ("S", [10]), [12], [0]),
+    (0, ("P", [4]), [0], [3]), (1, ("P", [6]), [0], [3]),
+    (0, ("S", [0, 1, 2, 3]), [8, 9, 10, 11], [2, 4, 6, 8]), (1, ("P", [3, 5, 7, 9]), [8, 9, 10, 11], [2, 4, 6, 8]),
+    (0, ("P", [1, 2]), [2, 3], [3, 5]), (1, ("S", [5, 6]), [2, 3], [3, 5]),
+    (1, ("S", [8]), [1], [1]), (0, ("S", [4, 12]), [1, 5], [1, 2]),
+    (0, ("P", [3]), [6], [7]), (1, ("P", [0, 6]), [5, 6], [2, 7]),
+]
+MERGE = [
+    (0, ("S", [13, 14, 15, 16], 0), ("S", [0, 4, 8, 12], 0), ("P", [9, 6, 3, 0], 1)),
+    (0, ("Y", [0, 1, 2, 3], 0), ("S", [12, 8, 4, 0], 1), ("P", [0, 3, 6, 9], 0)),
+    (1, ("S", [0, 1], 0), ("S", [13, 14], 0), ("Y", [0, 1], 0)), (1, ("P", [0, 1], 0), ("S", [15, 16], 0), ("Y", [2, 3], 0)),
+    (0, ("S", [2, 3], 0), ("S", [13, 14], 0), ("Y", [0, 1], 0)), (0, ("P", [2, 3], 0), ("S", [15, 16], 0), ("Y", [2, 3], 0)),
+    (1, ("S", [4, 6], 0), ("S", [0, 2], 0), ("P", [0, 2], 0)), (1, ("P", [4, 6], 0), ("S", [1, 3], 0), ("P", [1, 3], 0)),
+    (0, ("S", [5, 7], 0), ("S", [0, 2], 0), ("P", [0, 2], 0)), (0, ("P", [5, 7], 0), ("S", [1, 3], 0), ("P", [1, 3], 0)),
+    (1, ("F", [0, 2, 4, 6], 0), ("S", [4, 5, 6, 7], 0), ("P", [4, 5, 6, 7], 0)),
+    (0, ("F", [1, 3, 5, 7], 0), ("S", [4, 5, 6, 7], 0), ("P", [4, 5, 6, 7], 0)),
+]
+
+
+def sl(a, n, st=1):
+    e = a + st * (n - 1) + (1 if st > 0 else -1)
+    return slice(a, e if e >= 0 else None, st)
+
+
+def build_ops(cfg):
+    ops = []
+    tag = ["i"]
+    H = cfg["H"]
+    ch, lh = C // H, L // H
+    SC = scratch(H)
+
+    def op(eng, emit, rd, wr, cost, lat=0.0, kind="c"):
+        ops.append({"tag": tag[0], "eng": eng, "emit": emit, "rd": rd, "wr": wr, "cost": cost, "lat": lat, "kind": kind})
+        return len(ops) - 1
+
+    def size(a):
+        return int(np.zeros(SC[a[0]][1][1:], np.int8)[a[1:]].size)
+
+    def psum(a):
+        return SC[a[0]][0] == "psum"
+
+    def two(a):
+        return SC[a[0]][2] in ("bfloat16", "uint16")
+
+    def vcost(n):
+        return 55 + CY * max(n, 50)
+
+    def tt(o, a, b, alu):
+        n = size(o) * (1 if psum(a) or psum(b) else 2)
+        op("V", lambda x: x["V"].tensor_tensor(x["ap"](o), x["ap"](a), x["ap"](b), alu), [a, b], [o], vcost(n))
+
+    def ts(o, a, s1, s2, o0, o1=None):
+        n = size(o) * (0.5 if two(o) and two(a) else 1)
+        cs = [s for s in (s1, s2) if isinstance(s, tuple)]
+
+        def emit(x):
+            v1 = x["ap"](s1) if isinstance(s1, tuple) else s1
+            v2 = x["ap"](s2) if isinstance(s2, tuple) else s2
+            if o1 is None:
+                return x["V"].tensor_scalar(x["ap"](o), x["ap"](a), v1, None, o0)
+            return x["V"].tensor_scalar(x["ap"](o), x["ap"](a), v1, v2, o0, o1)
+        op("V", emit, [a] + cs, [o], vcost(n))
+
+    def cp(o, a):
+        n = size(o) * (0.5 if two(o) and two(a) else 1)
+        op("V", lambda x: x["V"].tensor_copy(x["ap"](o), x["ap"](a)), [a], [o], vcost(n))
+
+    def fill(o, v):
+        op("V", lambda x: x["V"].memset(x["ap"](o), v), [], [o], vcost(size(o) * (0.5 if two(o) else 1)))
+
+    def act(o, a, f, scale=1.0, bias=None):
+        if bias is None:
+            op("S", lambda x: x["S"].activation(x["ap"](o), x["ap"](a), f, scale=scale), [a], [o], 70 + CY * size(o))
+        else:
+            op("S", lambda x: x["S"].activation(x["ap"](o), x["ap"](a), f, bias=x["ap"](bias), scale=scale),
+               [a, bias], [o], 70 + CY * size(o))
+
+    def gather(eng, o, win, of, scale=1.0, minus=None):
+        wa = (win, ALL)
+        if eng == "S":
+            op("S", lambda x: x["S"].activation(x["ap"](o), x["ap"](wa).indirect(x["ap"](of)), ACT.Copy, scale=scale),
+               [wa, of], [o], 70 + CY * GA * size(o))
+        elif minus is None:
+            op("V", lambda x: x["V"].tensor_copy(x["ap"](o), x["ap"](wa).indirect(x["ap"](of))), [wa, of], [o], 55 + CY * GA * size(o))
+        else:
+            op("V", lambda x: x["V"].tensor_tensor(x["ap"](o), x["ap"](wa).indirect(x["ap"](of)), x["ap"](minus), ALU.subtract),
+               [wa, of, minus], [o], 55 + CY * GA * size(o))
+
+    def mm(items, f32=False):
+        def emit(x):
+            for o, w, r, st, sp in items:
+                last = x["P"].matmul(x["ap"](o), x["ap"](w), x["ap"](r), st, sp)
+            return last
+        cost = sum(max(64, size(it[2])) for it in items) * PE * (4 if f32 else 1)
+        outs = [it[0] for it in items]
+        edge = any(it[3] or it[4] for it in items)
+        op("P", emit, [it[1] for it in items] + [it[2] for it in items] + ([] if edge else outs), outs if edge else [], cost, 60.0)
+
+    def dma(eng, o, a, nbytes, add=False):
+        def emit(x):
+            if add:
+                return x["G"].dma_start(x["ap"](o), x["ap"](a), accum_op=ALU.add)
+            return x[eng].dma_start(x["ap"](o), x["ap"](a))
+        op(eng, emit, ([a] if a[0] in SC else []) + ([o] if add else []), [o] if o[0] in SC else [],
+           700.0 if eng == "G" else 80.0, 1900.0 + nbytes * 128 * (2 if add else 1) / 450.0, "dma")
+
+    def send(src, dst, nbytes):
+        i = op("G", None, [src], [], 500.0, 2500.0 + nbytes * 128 / 80.0, "send")
+        ops[i]["src"], ops[i]["dst"] = src, dst
+        j = op(None, None, [], [dst], 0.0, 0.0, "recv")
+        ops[j]["after"] = i
+
+    def gop(emit, rd, wr, n):
+        op("G", emit, rd, wr, 170 + 2 * CY * n)
+
+    def cols(b, a, n, st=1):
+        return (b, sl(a, n, st))
+
+    def mcol(j):
+        return cols("mc", j + 7, 1)
+
+    dma("Y", ("ndl", ALL), ("nd", ALL), 768)
+    dma("Y", ("pw", ALL), ("pa", ALL), 6144)
+    for q in range(4 * H):
+        dma("Y", ("fr", slice(0, H), sl(q * lh, lh)), cols("fc", 0, L), 768)
+    fill(("onesf", ALL), 1.0)
+    fill(("wm", ALL), 0.0)
+    fill(("wt", ALL), 65536.0)
+    gop(lambda x: x["G"].affine_select(x["ap"](("wt", ALL)), x["ap"](("wt", ALL)), [[-16, 8]], ALU.is_ge, 0.0, 0, 1),
+        [("wt", ALL)], [("wt", ALL)], 8)
+    gop(lambda x: x["G"].affine_select(x["ap"](cols("wm", 15, 8, 16)), x["ap"](("wt", ALL)), [[16, 8]], ALU.is_ge, 0.0, 15, -1),
+        [("wt", ALL)], [cols("wm", 15, 8, 16)], 8)
+    gop(lambda x: x["G"].affine_select(x["ap"](("idf", ALL)), x["ap"](("onesf", ALL)), [[-1, 128]], ALU.is_equal, 0.0, 0, 1),
+        [("onesf", ALL)], [("idf", ALL)], 128)
+    gop(lambda x: x["G"].iota(x["ap"](("t2", ALL)), [[4096, 16], [0, ch]], 0, 0, allow_small_or_imprecise_dtypes=True),
+        [], [("t2", ALL)], 16 * ch)
+
+    def lists(t, h, fa, fb, last=False):
+        m, n, x0 = "msg%d%d" % (t, h), K * ch, h * 256
+        pa_, pb_, co_ = (m, 0, 0), (m, 0, 1), (m, 0, 2)
+        of = cols("off%d" % h, t * 2 * n, n)
+        ts(pb_, fb, 0x38, None, ALU.bitwise_and)
+        ts(pa_, fa, 0xFF8, None, ALU.bitwise_and)
+        ts(cols("xp", x0, n), pb_, 0.125, -8.0 * t, ALU.mult, ALU.add)
+        tt(co_, pa_, cols("xp", x0, n), ALU.add)
+        cp(of, co_)
+        if not last:
+            send(of, cols("off%d" % h, t * 2 * n + n, n), 2 * n)
+            send((m, 0), (m, 1), 12 * n)
+            tt(cols("xp", x0 + n, n), pa_, cols("xp", x0, n), ALU.add)
+            tt(cols("xp", x0, n), pa_, cols("xp", x0, n), ALU.add)
+
+    for h in range(H):
+        nd_, tm_ = ("ndl", ALL, sl(h * ch, ch)), ("tmpi", ALL, sl(h * ch, ch))
+        ts(tm_, nd_, 8.0, 8.0, ALU.mult, ALU.add)
+        lists(0, h, nd_, tm_)
+    cp(("idb", ALL), ("idf", ALL))
+    ts(("big", ALL), ("idf", ALL), 2.0 ** 29, None, ALU.mult)
+    fill(("t1", ALL), -2.0 ** 27)
+    fill(("t3", ALL), 8.0)
+    dma("Y", ("eraw", ALL), ("ea", ALL), 6144)
+    dma("Y", ("xr", ALL), ("er", ALL), 3072)
+    dma("Y", ("dls", ALL), ("dl", ALL), 4)
+    for q in range(4 * H):
+        dma("Y", ("fr", slice(H, R * H), sl(q * lh, lh)), cols("fc", L, (R - 1) * L), 2304)
+    act(("hf", ALL), ("idf", ALL), ACT.Copy, -0.5)
+    for j in ([-2, 2] if "Q" not in cfg["chain"] else [-4, -3, -2, -1, 0, 1, 2, 4, 7]):
+        act(mcol(j), ("dls", ALL), ACT.Copy, float(j))
+    act(cols("ew", 1, 1535), cols("eraw", 0, 1535), ACT.Copy, -1.0)
+    act(cols("ew", 1536, 1536), cols("eraw", 1535, 1536), ACT.Copy, -1.0)
+    act(cols("ew", 0, L, 8), cols("eraw", 7, L, 8), ACT.Copy, -1.0)
+
+    def select(t, h):
+        m, kp, sfx = "msg%d%d" % (t, h), "kp%d" % h, "%d%d" % (t, h)
+        split = H == 1 and cfg["split"][t]
+
+        def wires(mem, pos, li):
+            s = sl(pos[0], len(pos), pos[1] - pos[0] if len(pos) > 1 else 1)
+            if mem == "Y":
+                return cols("xp", h * 256 + pos[0] * 2 * ch, len(pos) * 2 * ch)
+            if mem == "F":
+                return ("fin%d" % h, s, ALL)
+            if mem == "S":
+                return ("ss%d" % h, li, s, ALL)
+            return ("sp", slice(2 * h, 2 * h + 2) if li is ALL else 2 * h + li, s, ALL)
+
+        def cx(big, o, a, b):
+            tt(wires(*o), wires(*a), wires(*b), ALU.max if big else ALU.min)
+
+        def distances(li):
+            tag[0] = "oa"[li] + sfx
+            kl = (kp, li if H == 1 else ALL, ALL, slice(0, ch))
+            if H == 1 or li == 0:
+                mm([(kl, ("idb", ALL), ("t1", ALL), True, False), (kl, ("idb", ALL), cols("t2", li * 192, 192), False, False)])
+            for s0, s1, how in cfg["pieces"][t][h]:
+                if s0 // 8 != li:
+                    continue
+                n = (s1 - s0) * lh
+                d_, r_ = cols("dd%d" % h, s0 * lh, n), cols("rr%d" % h, s0 * lh, n)
+                of, ff = cols("off%d" % h, (t * 16 + s0) * ch, (s1 - s0) * ch), ("fr", t * H + h, slice(0, n))
+                if how in "SB":
+                    gather("S", d_, "pw", of, -1.0)
+                    dma("G", d_, ff, 2 * n, True)
+                else:
+                    gather("V", d_, "pw", of, minus=ff)
+                ko = (kp, li, slice(s0 % 8, s0 % 8 + s1 - s0), slice(0, ch))
+
+                def pas(buf):
+                    mm([(ko, cols("wm", 15 - r, 128), cols(buf, s0 * lh + r, n // 16, 16), False, False) for r in range(16)])
+                if how in "AB":
+                    act(r_, d_, ACT.Abs)
+                else:
+                    pas(d_[0])
+                    ts(r_, d_, 0.0, -2.0, ALU.min, ALU.mult)
+                pas(r_[0])
+            if li:
+                for r in range(K):
+                    tt(("eq%d" % h, r), (m, 1, 2), cols("xp", h * 256 + r * ch, K * ch), ALU.is_equal)
+                for r0 in (0, 4):
+                    mm([((kp, 1, ALL, slice(0, ch)), ("big", ALL), ("eq%d" % h, r), False, False) for r in range(r0, r0 + 4)])
+            if H == 1 or li == 1:
+                mm([(kl, ("idb", ALL), ("t3", ALL), False, True)])
+
+        def sort8(li):
+            tag[0] = "s" + sfx
+            for q in (0, 1):
+                for ab in (0, 1):
+                    o = wires("SP"[q], [0, 1, 2, 3], li)
+                    tt(o[:3] + (sl(ab * ch, ch),), (kp, li, sl(4 * q, 4), slice(0, ch)), (m, li, ab, sl(4 * q, 4), ALL), ALU.add)
+            for big, o, a, b in NET8:
+                cx(big, o + (li,), ("S", a, li), ("P", b, li))
+
+        distances(0)
+        if split:
+            sort8(0)
+        distances(1)
+        if t < R - 1 and h == H - 1:
+            for hh in range(H):
+                act(cols("pw", 8 * hh * lh + t, lh, 8), ("fr", t * H + hh, slice(0, lh)), ACT.Copy)
+        sort8(1 if split else ALL)
+        for c in MERGE:
+            cx(*c)
+        lists(t + 1, h, ("fin%d" % h, ALL, slice(0, ch)), ("fin%d" % h, ALL, slice(ch, 2 * ch)), t == R - 1)
+
+    def errors(t):
+        ga, bs = "ga%d" % t, "bs%d" % t
+        for q in range(4):
+            h, a, n = q * H // 4, q % (4 // H) * 2 * H, 2 * H
+            tag[0] = "g%d%d" % (t, h)
+            gather(cfg["egather"][t][q], (ga, h, sl(a * lh, n * lh)), "ew", cols("off%d" % h, ((t + 1) * 16 + a) * ch, n * ch))
+        nh = max(H, cfg["halves"][t])
+        n = L // nh
+        last, soft = t == R - 1, cfg["chain"][t] == "Q"
+
+        def bank(k, p):
+            return cols("bp%d" % ((nh * k + p) % 3), 0, n)
+
+        def gk(k, p):
+            return (ga, p * n // lh, sl(k * lh + p * n % lh, n))
+        for k in range(K + 1):
+            for p in range(nh):
+                tag[0] = "e%d%d" % (t, p * n // lh)
+                u, s_ = bank(k, p), cols("uu", p * n, n)
+                if k == 0:
+                    ts(s_, gk(0, p), mcol(2), mcol(-2), ALU.min, ALU.max)
+                elif k < K:
+                    mm([(u, ("idf", ALL), gk(k, p), True, False)], True)
+                    mm([(u, ("hf", ALL), s_, False, True)], True)
+                    if soft:
+                        act(cols("r1", p * n, n), u, ACT.Relu, -1.0, mcol(3 - k))
+                        act(u, cols("r1", p * n, n), ACT.Relu, -1.0, mcol(4))
+                    else:
+                        ts(u, u, mcol(2), mcol(-2), ALU.min, ALU.max)
+                    tt(s_, s_, u, ALU.add)
+                elif not soft:
+                    mm([(u, ("hf", ALL), s_, True, True)], True)
+                    if not last:
+                        tt(cols("ew", 8 * p * n + t + 1, n, 8), u, cols("xr", t * L + p * n, n), ALU.subtract)
+        b_ = (bs, ALL, slice(0, lh))
+        if soft:
+            act(b_, ("uu", ALL), ACT.Identity, -0.5, mcol(7))
+            tt(cols("ew", t + 1, L, 8), b_, cols("xr", t * L, L), ALU.subtract)
+        tag[0] = "p%d" % t
+        if last:
+            for k in range(K):
+                for p in range(nh):
+                    tt(gk(k, p), gk(k, p), bank(K, p), ALU.add)
+        if not soft:
+            act(b_, ("uu", ALL), ACT.Copy, -0.5)
+        dma("Y", cols("yb", t * L, L), b_, 1536)
+        if not last:
+            for q in range(1, 4):
+                dma("Y", (bs, ALL, sl(q * lh, lh)), b_, 1536)
+            for q in range(2):
+                dma("G", (ga, ALL, sl(q * 4 * lh, 4 * lh)), (bs, ALL), 6144, True)
+            for q in range(4):
+                g_ = (ga, ALL, sl(q * 2 * lh, 2 * lh))
+                act(g_, g_, ACT.Abs)
+                act(g_, g_, ACT.Exp, -1.0)
+            for n2 in (4 * lh, 2 * lh, lh):
+                dma("G", (ga, ALL, sl(0, n2)), (ga, ALL, sl(n2, n2)), 4 * n2 * H, True)
+            dma("Y", cols("ys", t * L, L), (ga, ALL, sl(0, lh)), 1536)
+        else:
+            sm = ("kp0", 0, slice(0, 6), ALL) if H == 1 else ("kp0", ALL, slice(0, 6), ALL)
+            for k in range(K):
+                g_ = (ga, ALL, sl(k * lh, lh))
+                if k >= K - cfg["vabs"]:
+                    ts(cols("xp", 0, L), g_, -1.0, None, ALU.mult)
+                    tt(g_, g_, cols("xp", 0, L), ALU.max)
+                else:
+                    act(g_, g_, ACT.Abs)
+                act(g_, g_, ACT.Exp, -1.0)
+                mm([(sm, ("idf", ALL), g_, k == 0, k == K - 1)], True)
+            cp(("so", ALL), sm)
+            dma("Y", cols("ys", t * L, L), ("so", ALL), 1536)
+
+    for t in range(R):
+        for h in range(H):
+            select(t, h)
+        errors(t)
+    return ops
+
+
+def analyse(cfg):
+    ops = build_ops(cfg)
+    SC = scratch(cfg["H"])
+    index = {b: np.arange(int(np.prod(v[1][1:]))).reshape(v[1][1:]) for b, v in SC.items()}
+    lastw = {b: np.full(index[b].size, -1) for b in SC}
+    readers = {b: [] for b in SC}
+    bank = {}
+    deps = []
+    for i, o in enumerate(ops):
+        d = set()
+        if "after" in o:
+            d.add(o["after"])
+        for a in o["rd"]:
+            e = index[a[0]][a[1:]].ravel()
+            d.update(int(v) for v in np.unique(lastw[a[0]][e]))
+        for a in o["wr"]:
+            e = index[a[0]][a[1:]].ravel()
+            d.update(int(v) for v in np.unique(lastw[a[0]][e]))
+            mask = np.zeros(index[a[0]].size, bool)
+            mask[e] = True
+            keep = []
+            for j, m in readers[a[0]]:
+                if np.any(m & mask):
+                    d.add(j)
+                if np.any(m & ~mask):
+                    keep.append((j, m & ~mask))
+            readers[a[0]] = keep
+        touched = set()
+        for a in o["rd"] + o["wr"]:
+            if SC[a[0]][0] == "psum":
+                touched.update((a[0], int(v)) for v in np.unique(index[a[0]][a[1:]] // 512))
+        for b in touched:
+            eng, js, before = bank.get(b, (o["eng"], [], []))
+            if eng != o["eng"]:
+                js, before = [], js
+            d.update(before)
+            bank[b] = (o["eng"], js + [i], before)
+        for a in o["rd"]:
+            mask = np.zeros(index[a[0]].size, bool)
+            mask[index[a[0]][a[1:]].ravel()] = True
+            readers[a[0]].append((i, mask))
+        for a in o["wr"]:
+            lastw[a[0]][index[a[0]][a[1:]].ravel()] = i
+        d.discard(-1)
+        d.discard(i)
+        deps.append(sorted(d))
+    return ops, deps
+
+
+def make_plan(cfg, known=None):
+    ops, deps = known or analyse(cfg)
+    n = len(ops)
+    succ = [[] for _ in range(n)]
+    for i in range(n):
+        for j in deps[i]:
+            succ[j].append(i)
+    prio = [0.0] * n
+    for i in range(n - 1, -1, -1):
+        prio[i] = ops[i]["cost"] + ops[i]["lat"] + max([prio[j] + HOP for j in succ[i]] + [0.0])
+    for i in range(n):
+        prio[i] += cfg["bias"].get(ops[i]["tag"], 0.0) * 1000
+    left = [len(d) for d in deps]
+    ready_at = [0.0] * n
+    done = [0.0] * n
+    free = {e: 0.0 for e in "VSPGY"}
+    order = {e: [] for e in "VSPGY"}
+    start = [0.0] * n
+    pool = [i for i in range(n) if left[i] == 0]
+
+    def finish(i, t):
+        done[i] = t
+        for j in succ[i]:
+            same = ops[i]["eng"] == ops[j]["eng"] == "P"
+            ready_at[j] = max(ready_at[j], t - ops[i]["lat"] if same else t + HOP)
+            left[j] -= 1
+            if left[j] == 0:
+                if ops[j]["eng"] is None:
+                    finish(j, ready_at[j])
+                else:
+                    pool.append(j)
+    while pool:
+        first = min(pool, key=lambda j: max(ready_at[j], free[ops[j]["eng"]]))
+        e = ops[first]["eng"]
+        t0 = max(ready_at[first], free[e])
+        i = max([j for j in pool if ops[j]["eng"] == e and ready_at[j] <= t0 + cfg["look"]], key=lambda j: (prio[j], -j))
+        pool.remove(i)
+        start[i] = max(ready_at[i], free[e])
+        free[e] = start[i] + ops[i]["cost"]
+        order[e].append(i)
+        finish(i, free[e] + ops[i]["lat"])
+    pos = {}
+    for e in order:
+        for p, i in enumerate(order[e]):
+            pos[i] = p
+    needed = set()
+    waits = {}
+    for e in order:
+        seen = {}
+        for i in order[e]:
+            w = {}
+            for j in deps[i]:
+                oj = ops[j]
+                if oj["kind"] == "c":
+                    if oj["eng"] == e == "P":
+                        continue
+                    key, val = oj["eng"], pos[j]
+                else:
+                    key, val = j, 0
+                if seen.get(key, -1) < val:
+                    w[key] = max(w.get(key, -1), val)
+            seen.update(w)
+            waits[i] = w
+            for key, val in w.items():
+                needed.add(order[key][val] if key in order else key)
+    count = {}
+    for e in order:
+        c = 0
+        for i in order[e]:
+            if ops[i]["kind"] == "c" and i in needed:
+                c += 1
+                count[i] = c
+    sems = {}
+    for i, o in enumerate(ops):
+        if o["kind"] != "c":
+            sems[i] = "d%d" % len(sems)
+    return {"ops": ops, "order": order, "waits": waits, "needed": needed, "count": count, "sems": sems,
+            "start": start, "done": done}
+
+
+def rank_program(g, core, T, topo):
+    rank = T.rank_of(core)
+    if rank is None:
+        return
+    if "p" not in PLAN:
+        PLAN["p"] = make_plan(CFG)
+    p = PLAN["p"]
+    ops, order, sems = p["ops"], p["order"], p["sems"]
+    dst = T.cores[(rank + 1) % len(T.cores)]
+    assert topo.may_write(core, dst)
+    rid, pid, _ = topo.addr(dst)
+    ne = 8
+    mask = sum(1 << e for e in topo.engines(core, dst)[:ne])
+    x = {"V": g.vector, "S": g.scalar, "P": g.tensor, "G": g, "Y": g.sync, "ap": lambda a: T[a[0]][(ALL,) + a[1:]]}
+    recv_of = {o["after"]: j for j, o in enumerate(ops) if o["kind"] == "recv"}
+    for e in "YGVSP":
+        q = x[e]
+        late = []
+        for i in order[e]:
+            o = ops[i]
+            for key, val in p["waits"][i].items():
+                if key in order:
+                    q.wait_ge(T.sem["c" + key], p["count"][order[key][val]])
+                else:
+                    q.wait_ge(T.sem[sems[key]], ne if ops[key]["kind"] == "recv" else 16)
+            if o["kind"] == "send":
+                g.remote_dma(x["ap"](o["dst"]), x["ap"](o["src"]), T.sem[sems[recv_of[i]]], T.sem[sems[i]], pid, rid, mask)
+                late.append((sems[i], ne))
+            elif o["kind"] == "dma":
+                o["emit"](x).then_inc(T.sem[sems[i]], 16)
+                if i not in p["needed"]:
+                    late.append((sems[i], 16))
+            else:
+                ins = o["emit"](x)
+                if i in p["needed"]:
+                    ins.then_inc(T.sem["c" + e], 1)
+        for s in late:
+            q.wait_ge(T.sem[s[0]], s[1])

@@ -8,14 +8,15 @@ CFG = {
     "split": [True] * 4,
     "halves": [2, 2, 2, 2],
 }
-CFG.update({'H': 1, 'split': [True, True, True, True], 'vabs': 2, 'chain': ['Q', 'P', 'P', 'P'], 'bias': {'s30': 2, 'o00': 58, 'e20': -5, 'g00': 1, 's00': 32, 'a00': 22, 'p0': -53, 'o30': 43, 'o10': 78, 'p3': -26, 'g10': -32, 'p2': -28, 's10': -13, 'e30': 102, 'p1': -34, 'a10': 38, 'o20': 46, 'a20': 25, 's20': -20, 'e10': -14, 'g20': 41, 'e00': 17, 'g30': -31, 'a30': -5}, 'pieces': [[[(0, 4, 'S'), (4, 8, 'V'), (8, 11, 'V'), (11, 14, 'B'), (14, 16, 'B')]], [[(0, 3, 'V'), (3, 5, 'S'), (5, 8, 'B'), (8, 10, 'B'), (10, 13, 'S'), (13, 16, 'V')]], [[(0, 2, 'S'), (2, 5, 'V'), (5, 8, 'B'), (8, 12, 'B'), (12, 14, 'S'), (14, 16, 'V')]], [[(0, 3, 'V'), (3, 6, 'S'), (6, 8, 'B'), (8, 11, 'B'), (11, 13, 'B'), (13, 16, 'B')]]], 'halves': [2, 2, 2, 2], 'egather': ['SVSS', 'SSSS', 'SSVS', 'VSVS'], 'look': 0})
+CFG.update({'pp': True, 'H': 2, 'pieces': [[[(0, 8, 'V'), (8, 16, 'V')], [(0, 8, 'B'), (8, 16, 'B')]], [[(0, 8, 'B'), (8, 16, 'S')], [(0, 8, 'B'), (8, 16, 'S')]], [[(0, 8, 'B'), (8, 16, 'S')], [(0, 8, 'B'), (8, 16, 'B')]], [[(0, 8, 'S'), (8, 16, 'S')], [(0, 8, 'B'), (8, 16, 'B')]]], 'halves': [2, 2, 2, 2], 'chain': ['P', 'P', 'P', 'P'], 'egather': ['XVSS', 'SSSS', 'SSSS', 'SSSV'], 'vabs': 1, 'look': 0, 'bias': {'o00': 7, 'a00': 6, 's00': 18, 'p0': -28, 'o10': 17, 'a10': 3, 's10': 27, 'p1': -67, 'o20': 8, 'a20': 10, 's20': 27, 'p2': -31, 'o30': 9, 'a30': 8, 's30': 29, 'e10': 5, 'g20': 21, 'a31': -6, 'o01': -11, 'a11': -1, 'g10': 3, 'g31': -20, 's31': -11, 'g01': -24, 'a21': -7, 'a01': -20, 'o11': 44, 'g00': -29, 'e11': -8, 'e00': 2, 's01': -1, 'g30': -3, 'e31': -5, 'e30': 23, 's21': 1, 'o31': -5, 'g21': 6, 'q0': 2, 'q1': 5}, 'turns': 2})
+CFG.update({'halves': [2, 2, 2, 4], 'pp': True, 'pieces': [[[(0, 8, 'A'), (8, 16, 'V')], [(0, 8, 'B'), (8, 12, 'B'), (12, 16, 'B')]], [[(0, 6, 'B'), (6, 8, 'V'), (8, 16, 'S')], [(0, 8, 'B'), (8, 16, 'B')]], [[(0, 8, 'S'), (8, 12, 'B'), (12, 16, 'S')], [(0, 3, 'S'), (3, 8, 'B'), (8, 11, 'B'), (11, 16, 'B')]], [[(0, 6, 'S'), (6, 8, 'B'), (8, 16, 'B')], [(0, 8, 'B'), (8, 16, 'B')]]], 'chain': ['P', 'P', 'P', 'P'], 'egather': ['SVSS', 'SSSS', 'SSSS', 'SSSX'], 'vabs': 1, 'look': 0, 'bias': {'o00': 19, 'a00': 4, 's00': 59, 'p0': 50, 'o10': 5, 'a10': 38, 's10': 19, 'p1': -11, 'o20': -44, 'a20': 10, 's20': 33, 'p2': -8, 'o30': 17, 'a30': -6, 's30': -18, 'e10': 9, 'g20': 52, 'a31': 5, 'o01': 34, 'a11': -15, 'g10': -35, 'g31': -18, 's31': 12, 'g01': -11, 'a21': -17, 'a01': -34, 'o11': -3, 'g00': -46, 'e11': 3, 'e00': 28, 's01': 1, 'g30': 10, 'e31': 36, 'e30': 12, 's21': 1, 'o31': -44, 'g21': -20, 'q0': 11, 'q1': -26, 'o21': -12, 'g11': -20, 's11': 28}, 'turns': 3, 'own': True})
 
 
 def scratch(H):
     ch, lh = C // H, L // H
     s = {
         "ndl": ("sbuf", [128, K, C], "int32"), "tmpi": ("sbuf", [128, K, C], "int32"),
-        "pw": ("sbuf", [128, W], "bfloat16"), "eraw": ("sbuf", [128, W], "bfloat16"), "ew": ("sbuf", [128, W], "float32"),
+        "pw": ("sbuf", [128, W], "bfloat16"), "pw1": ("sbuf", [128, W], "bfloat16"), "eraw": ("sbuf", [128, W], "bfloat16"), "ew": ("sbuf", [128, W], "float32"),
         "fr": ("sbuf", [128, R * H, 4 * L], "bfloat16"), "xr": ("sbuf", [128, R * L], "bfloat16"),
         "dls": ("sbuf", [128, 1], "float32"), "mc": ("sbuf", [128, 16], "float32"),
         "uu": ("sbuf", [128, L], "float32"), "r1": ("sbuf", [128, L], "float32"), "so": ("sbuf", [128, L], "float32"),
@@ -47,7 +48,11 @@ def scratch(H):
 SCRATCH = scratch(CFG["H"])
 SEMAPHORES = ["cV", "cS", "cP", "cG"] + ["d%d" % i for i in range(140)]
 
-CY, PE, GA, HOP = 1.04, 0.52, 1.56, 80.0
+CY, PE, GA, HOP = 1.04, 0.52, 1.56, 150.0
+OV, MN = 55.0, 50
+DG, DL, DB, GT, RL = 700.0, 1900.0, 450.0, 0.0, 2500.0
+RG, RB = 500.0, 80.0
+PM, PA = 2000.0, 0.0
 ALL = slice(None)
 PLAN = {}
 NET8 = [
@@ -91,7 +96,13 @@ def build_ops(cfg):
         return len(ops) - 1
 
     def size(a):
-        return int(np.zeros(SC[a[0]][1][1:], np.int8)[a[1:]].size)
+        n = 1
+        for j, d in enumerate(SC[a[0]][1][1:]):
+            if j + 1 >= len(a):
+                n *= d
+            elif isinstance(a[j + 1], slice):
+                n *= len(range(*a[j + 1].indices(d)))
+        return n
 
     def psum(a):
         return SC[a[0]][0] == "psum"
@@ -100,7 +111,7 @@ def build_ops(cfg):
         return SC[a[0]][2] in ("bfloat16", "uint16")
 
     def vcost(n):
-        return 55 + CY * max(n, 50)
+        return OV + CY * max(n, MN)
 
     def tt(o, a, b, alu):
         n = size(o) * (1 if psum(a) or psum(b) else 2)
@@ -138,10 +149,11 @@ def build_ops(cfg):
             op("S", lambda x: x["S"].activation(x["ap"](o), x["ap"](wa).indirect(x["ap"](of)), ACT.Copy, scale=scale),
                [wa, of], [o], 70 + CY * GA * size(o))
         elif minus is None:
-            op("V", lambda x: x["V"].tensor_copy(x["ap"](o), x["ap"](wa).indirect(x["ap"](of))), [wa, of], [o], 55 + CY * GA * size(o))
+            op("V", lambda x: x["V"].tensor_scalar(x["ap"](o), x["ap"](wa).indirect(x["ap"](of)), scale, None, ALU.mult),
+               [wa, of], [o], 55 + CY * GA * size(o))
         else:
             op("V", lambda x: x["V"].tensor_tensor(x["ap"](o), x["ap"](wa).indirect(x["ap"](of)), x["ap"](minus), ALU.subtract),
-               [wa, of, minus], [o], 55 + CY * GA * size(o))
+               [wa, of, minus], [o], 55 + CY * (GA + GT) * size(o))
 
     def mm(items, f32=False):
         def emit(x):
@@ -153,16 +165,16 @@ def build_ops(cfg):
         edge = any(it[3] or it[4] for it in items)
         op("P", emit, [it[1] for it in items] + [it[2] for it in items] + ([] if edge else outs), outs if edge else [], cost, 60.0)
 
-    def dma(eng, o, a, nbytes, add=False):
+    def dma(eng, o, a, nbytes, add=False, gate=()):
         def emit(x):
             if add:
                 return x["G"].dma_start(x["ap"](o), x["ap"](a), accum_op=ALU.add)
             return x[eng].dma_start(x["ap"](o), x["ap"](a))
-        op(eng, emit, ([a] if a[0] in SC else []) + ([o] if add else []), [o] if o[0] in SC else [],
-           700.0 if eng == "G" else 80.0, 1900.0 + nbytes * 128 * (2 if add else 1) / 450.0, "dma")
+        op(eng, emit, ([a] if a[0] in SC else []) + ([o] if add else []) + list(gate), [o] if o[0] in SC else [],
+           DG if eng == "G" else 80.0, DL + nbytes * 128 * (2 if add else 1) / DB + (PM if tag[0][0] == "p" else PA), "dma")
 
     def send(src, dst, nbytes):
-        i = op("G", None, [src], [], 500.0, 2500.0 + nbytes * 128 / 80.0, "send")
+        i = op("G", None, [src], [], RG, RL + nbytes * 128 / RB, "send")
         ops[i]["src"], ops[i]["dst"] = src, dst
         j = op(None, None, [], [dst], 0.0, 0.0, "recv")
         ops[j]["after"] = i
@@ -215,20 +227,32 @@ def build_ops(cfg):
     ts(("big", ALL), ("idf", ALL), 2.0 ** 29, None, ALU.mult)
     fill(("t1", ALL), -2.0 ** 27)
     fill(("t3", ALL), 8.0)
-    dma("Y", ("eraw", ALL), ("ea", ALL), 6144)
-    dma("Y", ("xr", ALL), ("er", ALL), 3072)
+    gate = [cols("off0", K * ch, K * ch)]
+    dma("G", cols("ew", 1, W - 1), cols("ea", 0, W - 1), 12288)
     dma("Y", ("dls", ALL), ("dl", ALL), 4)
-    for q in range(4 * H):
-        dma("Y", ("fr", slice(H, R * H), sl(q * lh, lh)), cols("fc", L, (R - 1) * L), 2304)
+    dma("Y", ("fr", slice(H, R * H), sl(0, lh)), cols("fc", L, (R - 1) * L), 2304)
+    dma("Y", ("eraw", ALL), ("ea", ALL), 6144, gate=gate)
+    dma("Y", ("xr", ALL), ("er", ALL), 3072, gate=gate)
+    n2 = lh
+    while n2 < 4 * L:
+        dma("Y", ("fr", slice(H, R * H), sl(n2, n2)), ("fr", slice(H, R * H), sl(0, n2)), 6 * H * n2)
+        n2 *= 2
     act(("hf", ALL), ("idf", ALL), ACT.Copy, -0.5)
     for j in ([-2, 2] if "Q" not in cfg["chain"] else [-4, -3, -2, -1, 0, 1, 2, 4, 7]):
         act(mcol(j), ("dls", ALL), ACT.Copy, float(j))
-    act(cols("ew", 1, 1535), cols("eraw", 0, 1535), ACT.Copy, -1.0)
-    act(cols("ew", 1536, 1536), cols("eraw", 1535, 1536), ACT.Copy, -1.0)
-    act(cols("ew", 0, L, 8), cols("eraw", 7, L, 8), ACT.Copy, -1.0)
+    act(cols("ew", 0, L, 8), cols("eraw", 7, L, 8), ACT.Copy)
+
+    def renew(pw, t):
+        for hh in range(H):
+            act(cols(pw, 8 * hh * lh + t, lh, 8), ("fr", t * H + hh, slice(0, lh)), ACT.Copy)
+
+    if cfg["pp"]:
+        dma("Y", ("pw1", ALL), ("pa", ALL), 6144, gate=gate)
+        renew("pw1", 0)
 
     def select(t, h):
         m, kp, sfx = "msg%d%d" % (t, h), "kp%d" % h, "%d%d" % (t, h)
+        pw = "pw1" if cfg["pp"] and t % 2 else "pw"
         split = H == 1 and cfg["split"][t]
 
         def wires(mem, pos, li):
@@ -256,10 +280,10 @@ def build_ops(cfg):
                 d_, r_ = cols("dd%d" % h, s0 * lh, n), cols("rr%d" % h, s0 * lh, n)
                 of, ff = cols("off%d" % h, (t * 16 + s0) * ch, (s1 - s0) * ch), ("fr", t * H + h, slice(0, n))
                 if how in "SB":
-                    gather("S", d_, "pw", of, -1.0)
+                    gather("S", d_, pw, of, -1.0)
                     dma("G", d_, ff, 2 * n, True)
                 else:
-                    gather("V", d_, "pw", of, minus=ff)
+                    gather("V", d_, pw, of, minus=ff)
                 ko = (kp, li, slice(s0 % 8, s0 % 8 + s1 - s0), slice(0, ch))
 
                 def pas(buf):
@@ -291,9 +315,9 @@ def build_ops(cfg):
         if split:
             sort8(0)
         distances(1)
-        if t < R - 1 and h == H - 1:
-            for hh in range(H):
-                act(cols("pw", 8 * hh * lh + t, lh, 8), ("fr", t * H + hh, slice(0, lh)), ACT.Copy)
+        if h == H - 1:
+            for t2 in ([t, t + 1] if t < R - 2 else []) if cfg["pp"] else ([t] if t < R - 1 else []):
+                renew(pw, t2)
         sort8(1 if split else ALL)
         for c in MERGE:
             cx(*c)
@@ -304,13 +328,24 @@ def build_ops(cfg):
         for q in range(4):
             h, a, n = q * H // 4, q % (4 // H) * 2 * H, 2 * H
             tag[0] = "g%d%d" % (t, h)
-            gather(cfg["egather"][t][q], (ga, h, sl(a * lh, n * lh)), "ew", cols("off%d" % h, ((t + 1) * 16 + a) * ch, n * ch))
+            how = cfg["egather"][t][q]
+            for eng, a0, n0 in ([(how, a, n)] if how != "X" else [("V", a, n // 2), ("S", a + n // 2, n // 2)]):
+                gather(eng, (ga, h, sl(a0 * lh, n0 * lh)), "ew", cols("off%d" % h, ((t + 1) * 16 + a0) * ch, n0 * ch), -1.0)
         nh = max(H, cfg["halves"][t])
         n = L // nh
         last, soft = t == R - 1, cfg["chain"][t] == "Q"
 
         def bank(k, p):
-            return cols("bp%d" % ((nh * k + p) % 3), 0, n)
+            if nh == 4:
+                return cols("bp%d" % p, 0, n) if p < 3 else ("kp1", 1, slice(0, 3), ALL)
+            if last and H == 2 and cfg["own"]:
+                return cols("bp%d" % (2 * p), 0, n) if k % 2 else (cols("bp1", 0, n) if p == 0 else ("kp1", 1, slice(0, 6), ALL))
+            if cfg.get("apart"):
+                return cols("bp%d" % (k % 2 if p == (t + cfg["apart"]) % 2 else 2), 0, n)
+            j = (nh * k + p) % (5 if last and H == 1 else 3)
+            if j == 3:
+                return ("kp0", 1, slice(0, n // 64), ALL)
+            return cols("bp%d" % j if j < 3 else "xp", 0, n)
 
         def gk(k, p):
             return (ga, p * n // lh, sl(k * lh + p * n % lh, n))
@@ -321,8 +356,15 @@ def build_ops(cfg):
                 if k == 0:
                     ts(s_, gk(0, p), mcol(2), mcol(-2), ALU.min, ALU.max)
                 elif k < K:
-                    mm([(u, ("idf", ALL), gk(k, p), True, False)], True)
-                    mm([(u, ("hf", ALL), s_, False, True)], True)
+                    if cfg["chain"][t] == "H":
+                        mm([(u, ("hf", ALL), s_, True, True)], True)
+                        tt(u, gk(k, p), u, ALU.add)
+                    elif cfg["chain"][t] == "Z":
+                        act(u, s_, ACT.Copy, -0.5)
+                        tt(u, gk(k, p), u, ALU.add)
+                    else:
+                        mm([(u, ("idf", ALL), gk(k, p), True, False)], True)
+                        mm([(u, ("hf", ALL), s_, False, True)], True)
                     if soft:
                         act(cols("r1", p * n, n), u, ACT.Relu, -1.0, mcol(3 - k))
                         act(u, cols("r1", p * n, n), ACT.Relu, -1.0, mcol(4))
@@ -332,12 +374,38 @@ def build_ops(cfg):
                 elif not soft:
                     mm([(u, ("hf", ALL), s_, True, True)], True)
                     if not last:
-                        tt(cols("ew", 8 * p * n + t + 1, n, 8), u, cols("xr", t * L + p * n, n), ALU.subtract)
+                        tt(cols("ew", 8 * p * n + t + 1, n, 8), cols("xr", t * L + p * n, n), u, ALU.subtract)
         b_ = (bs, ALL, slice(0, lh))
         if soft:
             act(b_, ("uu", ALL), ACT.Identity, -0.5, mcol(7))
-            tt(cols("ew", t + 1, L, 8), b_, cols("xr", t * L, L), ALU.subtract)
+            tt(cols("ew", t + 1, L, 8), cols("xr", t * L, L), b_, ALU.subtract)
         tag[0] = "p%d" % t
+        if last and H == 2:
+            for h in range(H):
+                tag[0] = "q%d" % h
+                sm, ng = ("kp%d" % h, 0, slice(0, 6), ALL), ("sp", 2 * h, slice(0, 8), ALL)
+                for k in range(K):
+                    for p in range(h * nh // 2, (h + 1) * nh // 2):
+                        tt(gk(k, p), gk(k, p), bank(K, p), ALU.add)
+                n = lh
+                act((bs, h), cols("uu", h * lh, lh), ACT.Copy, -0.5)
+                dma("Y", cols("yb", t * L + h * lh, lh), (bs, h), 768)
+                for k in range(0, K, 2):
+                    g_ = (ga, h, sl(k * lh, 2 * lh))
+                    if k >= K - cfg["vabs"]:
+                        for j in (k, k + 1):
+                            gj = (ga, h, sl(j * lh, lh))
+                            ts(ng, gj, -1.0, None, ALU.mult)
+                            tt(gj, gj, ng, ALU.max)
+                    else:
+                        act(g_, g_, ACT.Abs)
+                    act(g_, g_, ACT.Exp, -1.0)
+                    for j in range(k, min(k + 2, K - 1)):
+                        mm([(sm, ("idf", ALL), (ga, h, sl(j * lh, lh)), j == 0, j == K - 2)], True)
+                tt(cols("so", h * lh, lh), (ga, h, sl((K - 1) * lh, lh)), sm, ALU.add)
+                n = L // nh
+                dma("Y", cols("ys", t * L + h * lh, lh), cols("so", h * lh, lh), 768)
+            return
         if last:
             for k in range(K):
                 for p in range(nh):
@@ -346,8 +414,8 @@ def build_ops(cfg):
             act(b_, ("uu", ALL), ACT.Copy, -0.5)
         dma("Y", cols("yb", t * L, L), b_, 1536)
         if not last:
-            for q in range(1, 4):
-                dma("Y", (bs, ALL, sl(q * lh, lh)), b_, 1536)
+            dma("Y", (bs, ALL, sl(lh, lh)), b_, 1536)
+            dma("Y", (bs, ALL, sl(2 * lh, 2 * lh)), (bs, ALL, sl(0, 2 * lh)), 3072)
             for q in range(2):
                 dma("G", (ga, ALL, sl(q * 4 * lh, 4 * lh)), (bs, ALL), 6144, True)
             for q in range(4):
@@ -362,13 +430,15 @@ def build_ops(cfg):
             for k in range(K):
                 g_ = (ga, ALL, sl(k * lh, lh))
                 if k >= K - cfg["vabs"]:
-                    ts(cols("xp", 0, L), g_, -1.0, None, ALU.mult)
-                    tt(g_, g_, cols("xp", 0, L), ALU.max)
+                    ng = ("sp", 0, slice(0, 8 * H), ALL) if H == 1 else ("sp", slice(0, 2), slice(0, 8), ALL)
+                    ts(ng, g_, -1.0, None, ALU.mult)
+                    tt(g_, g_, ng, ALU.max)
                 else:
                     act(g_, g_, ACT.Abs)
                 act(g_, g_, ACT.Exp, -1.0)
-                mm([(sm, ("idf", ALL), g_, k == 0, k == K - 1)], True)
-            cp(("so", ALL), sm)
+                if k < K - 1:
+                    mm([(sm, ("idf", ALL), g_, k == 0, k == K - 2)], True)
+            tt(("so", ALL), g_, sm, ALU.add)
             dma("Y", cols("ys", t * L, L), ("so", ALL), 1536)
 
     for t in range(R):
@@ -439,35 +509,59 @@ def make_plan(cfg, known=None):
         prio[i] = ops[i]["cost"] + ops[i]["lat"] + max([prio[j] + HOP for j in succ[i]] + [0.0])
     for i in range(n):
         prio[i] += cfg["bias"].get(ops[i]["tag"], 0.0) * 1000
-    left = [len(d) for d in deps]
-    ready_at = [0.0] * n
-    done = [0.0] * n
-    free = {e: 0.0 for e in "VSPGY"}
-    order = {e: [] for e in "VSPGY"}
-    start = [0.0] * n
-    pool = [i for i in range(n) if left[i] == 0]
+    eng = [o["eng"] for o in ops]
+    cost = [o["cost"] for o in ops]
+    lat = [o["lat"] for o in ops]
 
-    def finish(i, t):
-        done[i] = t
-        for j in succ[i]:
-            same = ops[i]["eng"] == ops[j]["eng"] == "P"
-            ready_at[j] = max(ready_at[j], t - ops[i]["lat"] if same else t + HOP)
-            left[j] -= 1
-            if left[j] == 0:
-                if ops[j]["eng"] is None:
-                    finish(j, ready_at[j])
+    def run(prio, before, after, back):
+        left = [len(d) for d in before]
+        ready_at = [lat[i] if back else 0.0 for i in range(n)]
+        done = [0.0] * n
+        free = {e: 0.0 for e in "VSPGY"}
+        order = {e: [] for e in "VSPGY"}
+        start = [0.0] * n
+        pool = {e: [] for e in "VSPGY"}
+
+        def finish(i, t):
+            done[i] = t
+            for j in after[i]:
+                if eng[i] == eng[j] == "P":
+                    v = t if back else t - lat[i]
                 else:
-                    pool.append(j)
-    while pool:
-        first = min(pool, key=lambda j: max(ready_at[j], free[ops[j]["eng"]]))
-        e = ops[first]["eng"]
-        t0 = max(ready_at[first], free[e])
-        i = max([j for j in pool if ops[j]["eng"] == e and ready_at[j] <= t0 + cfg["look"]], key=lambda j: (prio[j], -j))
-        pool.remove(i)
-        start[i] = max(ready_at[i], free[e])
-        free[e] = start[i] + ops[i]["cost"]
-        order[e].append(i)
-        finish(i, free[e] + ops[i]["lat"])
+                    v = t + HOP + (lat[j] if back else 0.0)
+                if v > ready_at[j]:
+                    ready_at[j] = v
+                left[j] -= 1
+                if left[j] == 0:
+                    if eng[j] is None:
+                        finish(j, ready_at[j])
+                    else:
+                        pool[eng[j]].append(j)
+        for i in range(n):
+            if not before[i]:
+                pool[eng[i]].append(i)
+        while True:
+            t0, e = min([(max(free[e], min([ready_at[j] for j in pool[e]])), e) for e in pool if pool[e]] + [(1e30, "")])
+            if not e:
+                return order, start, done
+            i = max([(prio[j], -j) for j in pool[e] if ready_at[j] <= t0 + cfg["look"]])
+            i = -i[1]
+            pool[e].remove(i)
+            start[i] = max(ready_at[i], free[e])
+            free[e] = start[i] + cost[i]
+            order[e].append(i)
+            finish(i, free[e] + (0.0 if back else lat[i]))
+
+    order, start, done = run(prio, deps, succ, False)
+    last = done
+    rs = np.random.RandomState(cfg.get("seed", 0))
+    for _ in range(cfg.get("turns", 0)):
+        _, _, bd = run(last, succ, deps, True)
+        if cfg.get("seed"):
+            bd = [float(v) for v in np.array(bd) + cfg["noise"] * rs.rand(n)]
+        o2, s2, last = run(bd, deps, succ, False)
+        if max(last) < max(done):
+            order, start, done = o2, s2, last
     pos = {}
     for e in order:
         for p, i in enumerate(order[e]):

@@ -1,58 +1,65 @@
 import numpy as np
+from concourse.bass import DstId, RemoteDMATransfer
 from concourse.mybir import AluOpType as ALU, ActivationFunctionType as ACT
 
 L, K, R, W, C = 384, 8, 4, 3072, 24
+H = 2
+CH, LH = C // H, L // H
 
 CFG = {
-    "H": 1,
-    "split": [True] * 4,
-    "halves": [2, 2, 2, 2],
+    "slots": [[("AAAA", "VVVV"), ("SSBB", "BBBB")]] + [[("BBSS", "SSSS")] * 2] * 3,
+    "fold": 8,
+    "egather": ["ssss", "ssss", "ssss", "ssxx"],
+    "chain": ["0 0", "0 0", "0 0", "0 00"], "qadd": "VV",
+    "padd": "EEE", "psum": "DDV", "bc": 2, "co": "V", "nc": [4, 4], "run": 8,
+    "prel": "VVVVVSSS", "erel": "SSSSSSSS",
+    "vabs": [0, 2], "pabs": 0, "tries": 3500, "look": {"G": 600.0}, "share": 0.04, "move": 4000.0,
+    "gates": {"e": "m1", "p": "k00", "1": "k00", "x": "k01", "2": "k10", "3": "k20"},
 }
-CFG.update({'pp': True, 'H': 2, 'pieces': [[[(0, 8, 'V'), (8, 16, 'V')], [(0, 8, 'B'), (8, 16, 'B')]], [[(0, 8, 'B'), (8, 16, 'S')], [(0, 8, 'B'), (8, 16, 'S')]], [[(0, 8, 'B'), (8, 16, 'S')], [(0, 8, 'B'), (8, 16, 'B')]], [[(0, 8, 'S'), (8, 16, 'S')], [(0, 8, 'B'), (8, 16, 'B')]]], 'halves': [2, 2, 2, 2], 'chain': ['P', 'P', 'P', 'P'], 'egather': ['XVSS', 'SSSS', 'SSSS', 'SSSV'], 'vabs': 1, 'look': 0, 'bias': {'o00': 7, 'a00': 6, 's00': 18, 'p0': -28, 'o10': 17, 'a10': 3, 's10': 27, 'p1': -67, 'o20': 8, 'a20': 10, 's20': 27, 'p2': -31, 'o30': 9, 'a30': 8, 's30': 29, 'e10': 5, 'g20': 21, 'a31': -6, 'o01': -11, 'a11': -1, 'g10': 3, 'g31': -20, 's31': -11, 'g01': -24, 'a21': -7, 'a01': -20, 'o11': 44, 'g00': -29, 'e11': -8, 'e00': 2, 's01': -1, 'g30': -3, 'e31': -5, 'e30': 23, 's21': 1, 'o31': -5, 'g21': 6, 'q0': 2, 'q1': 5}, 'turns': 2})
-CFG.update({'halves': [2, 2, 2, 4], 'pp': True, 'pieces': [[[(0, 8, 'A'), (8, 16, 'V')], [(0, 8, 'B'), (8, 12, 'B'), (12, 16, 'B')]], [[(0, 6, 'B'), (6, 8, 'V'), (8, 16, 'S')], [(0, 8, 'B'), (8, 16, 'B')]], [[(0, 8, 'S'), (8, 12, 'B'), (12, 16, 'S')], [(0, 3, 'S'), (3, 8, 'B'), (8, 11, 'B'), (11, 16, 'B')]], [[(0, 6, 'S'), (6, 8, 'B'), (8, 16, 'B')], [(0, 8, 'B'), (8, 16, 'B')]]], 'chain': ['P', 'P', 'P', 'P'], 'egather': ['SVSS', 'SSSS', 'SSSS', 'SSSX'], 'vabs': 1, 'look': 0, 'bias': {'o00': 19, 'a00': 4, 's00': 59, 'p0': 50, 'o10': 5, 'a10': 38, 's10': 19, 'p1': -11, 'o20': -44, 'a20': 10, 's20': 33, 'p2': -8, 'o30': 17, 'a30': -6, 's30': -18, 'e10': 9, 'g20': 52, 'a31': 5, 'o01': 34, 'a11': -15, 'g10': -35, 'g31': -18, 's31': 12, 'g01': -11, 'a21': -17, 'a01': -34, 'o11': -3, 'g00': -46, 'e11': 3, 'e00': 28, 's01': 1, 'g30': 10, 'e31': 36, 'e30': 12, 's21': 1, 'o31': -44, 'g21': -20, 'q0': 11, 'q1': -26, 'o21': -12, 'g11': -20, 's11': 28}, 'turns': 3, 'own': True})
 
 
-def scratch(H):
-    ch, lh = C // H, L // H
+def scratch(cfg):
     s = {
-        "ndl": ("sbuf", [128, K, C], "int32"), "tmpi": ("sbuf", [128, K, C], "int32"),
-        "pw": ("sbuf", [128, W], "bfloat16"), "pw1": ("sbuf", [128, W], "bfloat16"), "eraw": ("sbuf", [128, W], "bfloat16"), "ew": ("sbuf", [128, W], "float32"),
-        "fr": ("sbuf", [128, R * H, 4 * L], "bfloat16"), "xr": ("sbuf", [128, R * L], "bfloat16"),
-        "dls": ("sbuf", [128, 1], "float32"), "mc": ("sbuf", [128, 16], "float32"),
-        "uu": ("sbuf", [128, L], "float32"), "r1": ("sbuf", [128, L], "float32"), "so": ("sbuf", [128, L], "float32"),
-        "wm": ("sbuf", [128, 144], "bfloat16"), "wt": ("sbuf", [128, 8], "bfloat16"),
+        "ndl": ("sbuf", [128, K, C], "int32"), "tb": ("sbuf", [128, K, C], "int32"), "tj": ("sbuf", [128, K, C], "int32"),
+        "tq": ("sbuf", [128, K, C], "int32"),
+        "praw": ("sbuf", [128, L, 8], "bfloat16"), "eraw": ("sbuf", [128, L, 8], "bfloat16"),
+        "pw0": ("sbuf", [128, 10 * L], "bfloat16"), "pw1": ("sbuf", [128, 10 * L], "bfloat16"), "ew": ("sbuf", [128, 11 * L], "float32"),
+        "fr": ("sbuf", [128, R * H, K * LH], "bfloat16"), "xr": ("sbuf", [128, R * L], "bfloat16"),
+        "dls": ("sbuf", [128, 1], "float32"), "mc": ("sbuf", [128, 2], "float32"),
+        "uu": ("sbuf", [128, 4, L], "float32"), "so": ("sbuf", [128, R, L], "float32"),
+        "w1": ("sbuf", [128, 144], "bfloat16"), "w2": ("sbuf", [128, 144], "bfloat16"), "wn": ("sbuf", [128, 144], "bfloat16"),
+        "wt": ("sbuf", [128, 8], "bfloat16"),
         "onesf": ("sbuf", [128, 128], "float32"), "idf": ("sbuf", [128, 128], "float32"), "hf": ("sbuf", [128, 128], "float32"),
-        "idb": ("sbuf", [128, 128], "bfloat16"), "big": ("sbuf", [128, 128], "bfloat16"),
-        "t1": ("sbuf", [128, 192], "bfloat16"), "t2": ("sbuf", [128, 16 * ch], "bfloat16"), "t3": ("sbuf", [128, 192], "bfloat16"),
+        "nf": ("sbuf", [128, 128], "float32"), "idb": ("sbuf", [128, 128], "bfloat16"), "big": ("sbuf", [128, 128], "bfloat16"),
+        "t2": ("sbuf", [128, 16 * CH], "bfloat16"),
     }
     for t in range(R):
-        s["ga%d" % t] = ("sbuf", [128, H, K * lh], "float32")
-        s["bs%d" % t] = ("sbuf", [128, H, (4 if t < R - 1 else 1) * lh], "float32")
+        s["ga%d" % t] = ("sbuf", [128, H, K * LH], "float32")
+        s["bs%d" % t] = ("sbuf", [128, H, (4 if t < R - 1 else 2) * LH], "float32")
     for h in range(H):
-        s["off%d" % h] = ("sbuf", [128, 5 * 16 * ch], "uint16")
-        for t in range(R + 1):
-            s["msg%d%d" % (t, h)] = ("sbuf", [128, 2, 3, K, ch], "int32")
-        s["dd%d" % h] = ("sbuf", [128, 16 * lh], "bfloat16")
-        s["rr%d" % h] = ("sbuf", [128, 16 * lh], "bfloat16")
-        s["eq%d" % h] = ("sbuf", [128, K, K * ch], "bfloat16")
-        s["ss%d" % h] = ("sbuf", [128, 2, 17, 2 * ch], "float32")
-        s["fin%d" % h] = ("sbuf", [128, K, 2 * ch], "int32")
+        s["off%d" % h] = ("sbuf", [128, 5 * 16 * CH], "uint16")
+        s["pay%d" % h] = ("sbuf", [128, R + 1, 2, K, 2 * CH], "int32")
+        s["co%d" % h] = ("sbuf", [128, R + 1, 2, K * CH], "float32")
+        s["dd%d" % h] = ("sbuf", [128, 16 * LH], "bfloat16")
+        s["rr%d" % h] = ("sbuf", [128, 16 * LH], "bfloat16")
+        s["eq%d" % h] = ("sbuf", [128, K, K * CH], "bfloat16")
+        s["ss%d" % h] = ("sbuf", [128, 2, 17, 2 * CH], "float32")
+        s["fin%d" % h] = ("sbuf", [128, K, 2 * CH], "int32")
     for h in range(H):
-        s["kp%d" % h] = ("psum", [128, 2, K, 64 // H], "float32")
+        s["kp%d" % h] = ("psum", [128, 2, K, 32], "float32")
     for b in ("xp", "bp0", "bp1", "bp2"):
         s[b] = ("psum", [128, 512], "float32")
-    s["sp"] = ("psum", [128, 2 * H, 10, 2 * ch], "float32")
+    s["sp"] = ("psum", [128, 2 * H, 10, 2 * CH], "float32")
     return s
 
 
-SCRATCH = scratch(CFG["H"])
-SEMAPHORES = ["cV", "cS", "cP", "cG"] + ["d%d" % i for i in range(140)]
+SCRATCH = scratch(CFG)
+SEMAPHORES = ["cV", "cS", "cP", "cG", "out"] + ["d%d" % i for i in range(144)]
 
-CY, PE, GA, HOP = 1.04, 0.52, 1.56, 150.0
-OV, MN = 55.0, 50
-DG, DL, DB, GT, RL = 700.0, 1900.0, 450.0, 0.0, 2500.0
-RG, RB = 500.0, 80.0
-PM, PA = 2000.0, 0.0
+COSTS = {"cy": 1.0, "ga": 1.7, "ov": 45.0, "mn": 50, "hop": 150.0, "same": 100.0,
+         "dg": 700.0, "dl": 1800.0, "db": 650.0, "rg": 900.0, "rl": 2000.0, "rb": 120.0, "fl": 4400.0, "fb": 400.0, "row": 12.0, "far": 30.0}
+JUDGES = [dict(COSTS, cy=0.83, ga=1.56), dict(COSTS, cy=1.1, ga=1.2), dict(COSTS, cy=1.15, ga=2.05, rg=1200.0, dl=2100.0),
+          dict(COSTS, cy=0.95, dg=1000.0, rg=1500.0, dl=2100.0, rl=2800.0, db=600.0, row=20.0, far=60.0)]
 ALL = slice(None)
 PLAN = {}
 NET8 = [
@@ -69,9 +76,9 @@ NET8 = [
 ]
 MERGE = [
     (0, ("S", [13, 14, 15, 16], 0), ("S", [0, 4, 8, 12], 0), ("P", [9, 6, 3, 0], 1)),
-    (0, ("Y", [0, 1, 2, 3], 0), ("S", [12, 8, 4, 0], 1), ("P", [0, 3, 6, 9], 0)),
-    (1, ("S", [0, 1], 0), ("S", [13, 14], 0), ("Y", [0, 1], 0)), (1, ("P", [0, 1], 0), ("S", [15, 16], 0), ("Y", [2, 3], 0)),
-    (0, ("S", [2, 3], 0), ("S", [13, 14], 0), ("Y", [0, 1], 0)), (0, ("P", [2, 3], 0), ("S", [15, 16], 0), ("Y", [2, 3], 0)),
+    (0, ("P", [0, 1, 2, 3], 1), ("S", [12, 8, 4, 0], 1), ("P", [0, 3, 6, 9], 0)),
+    (1, ("S", [0, 1], 0), ("S", [13, 14], 0), ("P", [0, 1], 1)), (1, ("P", [0, 1], 0), ("S", [15, 16], 0), ("P", [2, 3], 1)),
+    (0, ("S", [2, 3], 0), ("S", [13, 14], 0), ("P", [0, 1], 1)), (0, ("P", [2, 3], 0), ("S", [15, 16], 0), ("P", [2, 3], 1)),
     (1, ("S", [4, 6], 0), ("S", [0, 2], 0), ("P", [0, 2], 0)), (1, ("P", [4, 6], 0), ("S", [1, 3], 0), ("P", [1, 3], 0)),
     (0, ("S", [5, 7], 0), ("S", [0, 2], 0), ("P", [0, 2], 0)), (0, ("P", [5, 7], 0), ("S", [1, 3], 0), ("P", [1, 3], 0)),
     (1, ("F", [0, 2, 4, 6], 0), ("S", [4, 5, 6, 7], 0), ("P", [4, 5, 6, 7], 0)),
@@ -84,15 +91,24 @@ def sl(a, n, st=1):
     return slice(a, e if e >= 0 else None, st)
 
 
+def runs(s):
+    out = []
+    for i, c in enumerate(s):
+        if out and out[-1][0] == c:
+            out[-1][2] += 1
+        else:
+            out.append([c, i, 1])
+    return out
+
+
 def build_ops(cfg):
     ops = []
     tag = ["i"]
-    H = cfg["H"]
-    ch, lh = C // H, L // H
-    SC = scratch(H)
+    marks = {}
+    SC = scratch(cfg)
 
-    def op(eng, emit, rd, wr, cost, lat=0.0, kind="c"):
-        ops.append({"tag": tag[0], "eng": eng, "emit": emit, "rd": rd, "wr": wr, "cost": cost, "lat": lat, "kind": kind})
+    def op(eng, emit, rd, wr, work, kind="c", acc=(), **more):
+        ops.append(dict(more, tag=tag[0], eng=eng, emit=emit, rd=list(rd), wr=list(wr), acc=list(acc), work=work, kind=kind))
         return len(ops) - 1
 
     def size(a):
@@ -104,18 +120,21 @@ def build_ops(cfg):
                 n *= len(range(*a[j + 1].indices(d)))
         return n
 
+    def rows(a):
+        if a[0] not in SC:
+            return 1
+        e = np.arange(int(np.prod(SC[a[0]][1][1:]))).reshape(SC[a[0]][1][1:])[a[1:]].ravel()
+        return 1 + int(np.sum(np.diff(e) != 1))
+
     def psum(a):
         return SC[a[0]][0] == "psum"
 
     def two(a):
         return SC[a[0]][2] in ("bfloat16", "uint16")
 
-    def vcost(n):
-        return OV + CY * max(n, MN)
-
     def tt(o, a, b, alu):
         n = size(o) * (1 if psum(a) or psum(b) else 2)
-        op("V", lambda x: x["V"].tensor_tensor(x["ap"](o), x["ap"](a), x["ap"](b), alu), [a, b], [o], vcost(n))
+        op("V", lambda x: x["V"].tensor_tensor(x["ap"](o), x["ap"](a), x["ap"](b), alu), [a, b], [o], n)
 
     def ts(o, a, s1, s2, o0, o1=None):
         n = size(o) * (0.5 if two(o) and two(a) else 1)
@@ -127,138 +146,162 @@ def build_ops(cfg):
             if o1 is None:
                 return x["V"].tensor_scalar(x["ap"](o), x["ap"](a), v1, None, o0)
             return x["V"].tensor_scalar(x["ap"](o), x["ap"](a), v1, v2, o0, o1)
-        op("V", emit, [a] + cs, [o], vcost(n))
+        op("V", emit, [a] + cs, [o], n)
 
     def cp(o, a):
-        n = size(o) * (0.5 if two(o) and two(a) else 1)
-        op("V", lambda x: x["V"].tensor_copy(x["ap"](o), x["ap"](a)), [a], [o], vcost(n))
+        op("V", lambda x: x["V"].tensor_copy(x["ap"](o), x["ap"](a)), [a], [o], size(o) * (0.5 if two(o) and two(a) else 1))
 
     def fill(o, v):
-        op("V", lambda x: x["V"].memset(x["ap"](o), v), [], [o], vcost(size(o) * (0.5 if two(o) else 1)))
+        op("V", lambda x: x["V"].memset(x["ap"](o), v), [], [o], size(o) * (0.5 if two(o) else 1))
 
-    def act(o, a, f, scale=1.0, bias=None):
-        if bias is None:
-            op("S", lambda x: x["S"].activation(x["ap"](o), x["ap"](a), f, scale=scale), [a], [o], 70 + CY * size(o))
+    def act(o, a, f, scale=1.0):
+        op("S", lambda x: x["S"].activation(x["ap"](o), x["ap"](a), f, scale=scale), [a], [o], size(o))
+
+    def select(o, a, pattern, cmp, base, mult):
+        op("G", lambda x: x["G"].affine_select(x["ap"](o), x["ap"](a), pattern, cmp, 0.0, base, mult), [a], [o], 2 * size(o))
+
+    def move(eng, o, a):
+        if eng == "V":
+            cp(o, a)
+        elif eng == "S":
+            act(o, a, ACT.Copy)
         else:
-            op("S", lambda x: x["S"].activation(x["ap"](o), x["ap"](a), f, bias=x["ap"](bias), scale=scale),
-               [a, bias], [o], 70 + CY * size(o))
+            select(o, a, [[0, size(o)]], ALU.is_ge, 0, 0)
 
-    def gather(eng, o, win, of, scale=1.0, minus=None):
-        wa = (win, ALL)
+    def gather(eng, o, wa, of, scale=1.0, minus=None):
         if eng == "S":
             op("S", lambda x: x["S"].activation(x["ap"](o), x["ap"](wa).indirect(x["ap"](of)), ACT.Copy, scale=scale),
-               [wa, of], [o], 70 + CY * GA * size(o))
+               [wa, of], [o], size(o), "g")
         elif minus is None:
             op("V", lambda x: x["V"].tensor_scalar(x["ap"](o), x["ap"](wa).indirect(x["ap"](of)), scale, None, ALU.mult),
-               [wa, of], [o], 55 + CY * GA * size(o))
+               [wa, of], [o], size(o), "g")
         else:
             op("V", lambda x: x["V"].tensor_tensor(x["ap"](o), x["ap"](wa).indirect(x["ap"](of)), x["ap"](minus), ALU.subtract),
-               [wa, of, minus], [o], 55 + CY * (GA + GT) * size(o))
+               [wa, of, minus], [o], size(o), "g")
 
-    def mm(items, f32=False):
+    def mm(group, items, start=False):
         def emit(x):
-            for o, w, r, st, sp in items:
-                last = x["P"].matmul(x["ap"](o), x["ap"](w), x["ap"](r), st, sp)
+            for j, (o, w, r) in enumerate(items):
+                last = x["P"].matmul(x["ap"](o), x["ap"](w), x["ap"](r), start and j == 0, x["stop"] and j == len(items) - 1)
             return last
-        cost = sum(max(64, size(it[2])) for it in items) * PE * (4 if f32 else 1)
+        n = sum(max(64, size(it[2])) * (0.5 if two(it[2]) else 2) for it in items)
         outs = [it[0] for it in items]
-        edge = any(it[3] or it[4] for it in items)
-        op("P", emit, [it[1] for it in items] + [it[2] for it in items] + ([] if edge else outs), outs if edge else [], cost, 60.0)
+        op("P", emit, [it[1] for it in items] + [it[2] for it in items], outs[:1] if start else [], n,
+           acc=outs[1:] if start else outs, group=group)
 
-    def dma(eng, o, a, nbytes, add=False, gate=()):
+    def dma(eng, o, a, nbytes, add=False, gate=None):
         def emit(x):
             if add:
                 return x["G"].dma_start(x["ap"](o), x["ap"](a), accum_op=ALU.add)
             return x[eng].dma_start(x["ap"](o), x["ap"](a))
-        op(eng, emit, ([a] if a[0] in SC else []) + ([o] if add else []) + list(gate), [o] if o[0] in SC else [],
-           DG if eng == "G" else 80.0, DL + nbytes * 128 * (2 if add else 1) / DB + (PM if tag[0][0] == "p" else PA), "dma")
+        op(eng, emit, ([a] if a[0] in SC else []) + ([o] if add else []), [o] if o[0] in SC else [],
+           nbytes * 128 * (2 if add else 1), "dma", rows=8 * max(rows(o), rows(a)), **({} if gate is None else {"after": gate}))
 
-    def send(src, dst, nbytes):
-        i = op("G", None, [src], [], RG, RL + nbytes * 128 / RB, "send")
-        ops[i]["src"], ops[i]["dst"] = src, dst
-        j = op(None, None, [], [dst], 0.0, 0.0, "recv")
-        ops[j]["after"] = i
+    def send(pairs, nbytes):
+        i = op("G", None, [p[0] for p in pairs], [], nbytes * 128, "send", pairs=pairs, behind=marks.get("sent"))
+        marks["sent"] = i
+        op(None, None, [], [p[1] for p in pairs], 0, "recv", after=i)
 
-    def gop(emit, rd, wr, n):
-        op("G", emit, rd, wr, 170 + 2 * CY * n)
+    def fold(pairs, back, alu, nbytes):
+        srcs = [s for p in pairs for s in p[0]]
+        i = op("G", None, srcs, [], nbytes * 128, "fold", pairs=pairs, alu=alu, back=back)
+        op(None, None, srcs, [back], 0, "recv", after=i)
 
     def cols(b, a, n, st=1):
         return (b, sl(a, n, st))
 
-    def mcol(j):
-        return cols("mc", j + 7, 1)
-
     dma("Y", ("ndl", ALL), ("nd", ALL), 768)
-    dma("Y", ("pw", ALL), ("pa", ALL), 6144)
-    for q in range(4 * H):
-        dma("Y", ("fr", slice(0, H), sl(q * lh, lh)), cols("fc", 0, L), 768)
+    dma("Y", ("praw", ALL), ("pa", ALL), 6144)
+    for q in range(4):
+        dma("Y", ("fr", slice(0, H), sl(q * LH, LH)), cols("fc", 0, L), 768)
     fill(("onesf", ALL), 1.0)
-    fill(("wm", ALL), 0.0)
-    fill(("wt", ALL), 65536.0)
-    gop(lambda x: x["G"].affine_select(x["ap"](("wt", ALL)), x["ap"](("wt", ALL)), [[-16, 8]], ALU.is_ge, 0.0, 0, 1),
-        [("wt", ALL)], [("wt", ALL)], 8)
-    gop(lambda x: x["G"].affine_select(x["ap"](cols("wm", 15, 8, 16)), x["ap"](("wt", ALL)), [[16, 8]], ALU.is_ge, 0.0, 15, -1),
-        [("wt", ALL)], [cols("wm", 15, 8, 16)], 8)
-    gop(lambda x: x["G"].affine_select(x["ap"](("idf", ALL)), x["ap"](("onesf", ALL)), [[-1, 128]], ALU.is_equal, 0.0, 0, 1),
-        [("onesf", ALL)], [("idf", ALL)], 128)
-    gop(lambda x: x["G"].iota(x["ap"](("t2", ALL)), [[4096, 16], [0, ch]], 0, 0, allow_small_or_imprecise_dtypes=True),
-        [], [("t2", ALL)], 16 * ch)
-
-    def lists(t, h, fa, fb, last=False):
-        m, n, x0 = "msg%d%d" % (t, h), K * ch, h * 256
-        pa_, pb_, co_ = (m, 0, 0), (m, 0, 1), (m, 0, 2)
-        of = cols("off%d" % h, t * 2 * n, n)
-        ts(pb_, fb, 0x38, None, ALU.bitwise_and)
-        ts(pa_, fa, 0xFF8, None, ALU.bitwise_and)
-        ts(cols("xp", x0, n), pb_, 0.125, -8.0 * t, ALU.mult, ALU.add)
-        tt(co_, pa_, cols("xp", x0, n), ALU.add)
-        cp(of, co_)
-        if not last:
-            send(of, cols("off%d" % h, t * 2 * n + n, n), 2 * n)
-            send((m, 0), (m, 1), 12 * n)
-            tt(cols("xp", x0 + n, n), pa_, cols("xp", x0, n), ALU.add)
-            tt(cols("xp", x0, n), pa_, cols("xp", x0, n), ALU.add)
-
-    for h in range(H):
-        nd_, tm_ = ("ndl", ALL, sl(h * ch, ch)), ("tmpi", ALL, sl(h * ch, ch))
-        ts(tm_, nd_, 8.0, 8.0, ALU.mult, ALU.add)
-        lists(0, h, nd_, tm_)
-    cp(("idb", ALL), ("idf", ALL))
-    ts(("big", ALL), ("idf", ALL), 2.0 ** 29, None, ALU.mult)
-    fill(("t1", ALL), -2.0 ** 27)
-    fill(("t3", ALL), 8.0)
-    gate = [cols("off0", K * ch, K * ch)]
-    dma("G", cols("ew", 1, W - 1), cols("ea", 0, W - 1), 12288)
-    dma("Y", ("dls", ALL), ("dl", ALL), 4)
-    dma("Y", ("fr", slice(H, R * H), sl(0, lh)), cols("fc", L, (R - 1) * L), 2304)
-    dma("Y", ("eraw", ALL), ("ea", ALL), 6144, gate=gate)
-    dma("Y", ("xr", ALL), ("er", ALL), 3072, gate=gate)
-    n2 = lh
-    while n2 < 4 * L:
-        dma("Y", ("fr", slice(H, R * H), sl(n2, n2)), ("fr", slice(H, R * H), sl(0, n2)), 6 * H * n2)
-        n2 *= 2
+    fill(("w1", ALL), 0.0)
+    fill(("wt", ALL), 1024.0)
+    select(("wt", ALL), ("wt", ALL), [[-16, 8]], ALU.is_ge, 0, 1)
+    select(cols("w1", 15, 8, 16), ("wt", ALL), [[16, 8]], ALU.is_ge, 15, -1)
+    select(("idf", ALL), ("onesf", ALL), [[-1, 128]], ALU.is_equal, 0, 1)
+    op("G", lambda x: x["G"].iota(x["ap"](("t2", ALL)), [[64, 16], [0, CH]], 0, 0, allow_small_or_imprecise_dtypes=True),
+       [], [("t2", ALL)], 32 * CH)
+    if any(c in "sv" for day in cfg["slots"] for half in day for s in half for c in s):
+        act(("w2", ALL), ("w1", ALL), ACT.Copy, 2.0)
+        act(("wn", ALL), ("w1", ALL), ACT.Copy, -1.0)
+    act(("idb", ALL), ("idf", ALL), ACT.Copy)
+    act(("big", ALL), ("idf", ALL), ACT.Copy, 2.0 ** 23)
     act(("hf", ALL), ("idf", ALL), ACT.Copy, -0.5)
-    for j in ([-2, 2] if "Q" not in cfg["chain"] else [-4, -3, -2, -1, 0, 1, 2, 4, 7]):
-        act(mcol(j), ("dls", ALL), ACT.Copy, float(j))
-    act(cols("ew", 0, L, 8), cols("eraw", 7, L, 8), ACT.Copy)
 
-    def renew(pw, t):
-        for hh in range(H):
-            act(cols(pw, 8 * hh * lh + t, lh, 8), ("fr", t * H + hh, slice(0, lh)), ACT.Copy)
+    def hand_on(t, h):
+        n, pay, co = K * CH, "pay%d" % h, "co%d" % h
+        if cfg["co"] == "M":
+            send([((pay, t, 0, sl(0, 4)), (pay, t, 1, sl(0, 4))), ((pay, t, 0, sl(4, 4)), (pay, t, 1, sl(4, 4))), ((co, t, 0), (co, t, 1))], 12 * n)
+        else:
+            send([((pay, t, 0), (pay, t, 1))], 8 * n)
+        tag[0] = "v%d%d" % (t, h)
+        if cfg["co"] == "V":
+            cp((co, t, 1), offsets(t, h, 1))
+        mm("x%d%da" % (t, h), [(cols("xp", h * 256, n), ("idf", ALL), (co, t, 0))], True)
+        mm("x%d%db" % (t, h), [(cols("xp", h * 256 + n, n - CH), ("idf", ALL), (co, t, 0, slice(0, n - CH)))], True)
+        for r in range(K):
+            tt(("eq%d" % h, r), (co, t, 1), cols("xp", h * 256 + r * CH, n), ALU.is_equal)
+        tag[0] = "i"
 
-    if cfg["pp"]:
-        dma("Y", ("pw1", ALL), ("pa", ALL), 6144, gate=gate)
-        renew("pw1", 0)
+    def offsets(t, h, li, first=0, n=K):
+        return cols("off%d" % h, (t * 16 + li * K + first) * CH, n * CH)
 
-    def select(t, h):
-        m, kp, sfx = "msg%d%d" % (t, h), "kp%d" % h, "%d%d" % (t, h)
-        pw = "pw1" if cfg["pp"] and t % 2 else "pw"
-        split = H == 1 and cfg["split"][t]
+    ts(("tb", ALL), ("ndl", ALL), 7, None, ALU.bitwise_and)
+    ts(("tj", ALL), ("ndl", ALL), 3, None, ALU.arith_shift_right)
+    for h in range(H):
+        half, tmp = (ALL, sl(h * CH, CH)), ("sp", 2 * h + 1, slice(4, 8), ALL)
+        ts(tmp, ("tb",) + half, float(L), None, ALU.mult)
+        tt(("tq",) + half, ("tj",) + half, tmp, ALU.add)
+        cp(offsets(0, h, 0), ("tq",) + half)
+        send([(offsets(0, h, 0), offsets(0, h, 1))], 2 * K * CH)
+        marks["m%d" % h] = len(ops) - 1
+        ts(("pay%d" % h, 0, 0, ALL, slice(0, CH)), ("tq",) + half, 6, None, ALU.arith_shift_right)
+        ts(("pay%d" % h, 0, 0, ALL, slice(CH, 2 * CH)), ("tq",) + half, 63, None, ALU.bitwise_and)
+        cp(("co%d" % h, 0, 0), ("tq",) + half)
+        hand_on(0, h)
+    for b in range(8):
+        move(cfg["prel"][b], cols("pw0", b * L, L), ("praw", ALL, (b + 1) % 8))
+
+    def loads(mark):
+        gate, keep = marks.get(mark), tag[0]
+        tag[0] = "l" + mark
+        for what in [w for w in sorted(cfg["gates"]) if cfg["gates"][w] == mark]:
+            if what == "e":
+                dma("Y", ("eraw", ALL), ("ea", ALL), 6144, gate=gate)
+                dma("Y", ("dls", ALL), ("dl", ALL), 4, gate=gate)
+                for j in range(2):
+                    act(cols("mc", j, 1), ("dls", ALL), ACT.Copy, 4.0 * j - 2.0)
+                for b in range(8):
+                    move(cfg["erel"][b], cols("ew", b * L, L), ("eraw", ALL, (b + 1) % 8))
+            elif what == "p":
+                dma("Y", cols("pw1", 0, 6 * L), cols("pw0", L, 6 * L), 12 * L, gate=gate)
+                dma("Y", cols("pw1", 7 * L, L), cols("pw0", 0, L), 2 * L, gate=gate)
+                dma("Y", cols("pw1", 6 * L, L), cols("fc", 0, L), 2 * L, gate=gate)
+            elif what == "x":
+                dma("Y", ("xr", ALL), ("er", ALL), 3072, gate=gate)
+                dma("Y", cols("ew", 8 * L, 3 * L), cols("ew", 0, 3 * L), 12 * L, gate=gate)
+                for t in (2, 3):
+                    dma("Y", cols("pw%d" % (t % 2), 9 * L, L), cols("pw0", (t - 1) * L, L), 2 * L, gate=gate)
+                    dma("Y", cols("pw%d" % (t % 2), 8 * L, L), cols("fc", (t - 1) * L, L), 2 * L, gate=gate)
+            else:
+                rows, n2 = sl(int(what) * H, H), LH
+                dma("Y", ("fr", rows, sl(0, LH)), cols("fc", int(what) * L, L), 2 * L, gate=gate)
+                while n2 < max(cfg["nc"]) * LH:
+                    dma("Y", ("fr", rows, sl(n2, n2)), ("fr", rows, sl(0, n2)), 2 * H * n2)
+                    n2 *= 2
+        tag[0] = keep
+
+    for m in ("", "m0", "m1"):
+        loads(m)
+
+    def choice(t, h):
+        kp, dd, rr, pay, co, sfx = "kp%d" % h, "dd%d" % h, "rr%d" % h, "pay%d" % h, "co%d" % h, "%d%d" % (t, h)
+        win = cols("pw%d" % (t % 2), (t - t % 2) * L, W)
+        folded = any(c in "sv" for s in cfg["slots"][t][h] for c in s)
 
         def wires(mem, pos, li):
             s = sl(pos[0], len(pos), pos[1] - pos[0] if len(pos) > 1 else 1)
-            if mem == "Y":
-                return cols("xp", h * 256 + pos[0] * 2 * ch, len(pos) * 2 * ch)
             if mem == "F":
                 return ("fin%d" % h, s, ALL)
             if mem == "S":
@@ -268,215 +311,247 @@ def build_ops(cfg):
         def cx(big, o, a, b):
             tt(wires(*o), wires(*a), wires(*b), ALU.max if big else ALU.min)
 
-        def distances(li):
+        def pas(w, src, s0, ns):
+            ko = (kp, s0 // K, sl(s0 % K, ns), slice(0, CH))
+            for r0 in range(0, 16, cfg["run"]):
+                mm("k" + sfx, [(ko, cols(w, 15 - r, 128), src[:-1] + (sl(src[-1].start + r, ns * CH, 16),)) for r in range(r0, r0 + cfg["run"])])
+
+        tag[0] = "o" + sfx
+        mm("k" + sfx, [((kp, ALL, ALL, slice(0, CH)), ("idb", ALL), ("t2", ALL))], True)
+        for li in range(2):
             tag[0] = "oa"[li] + sfx
-            kl = (kp, li if H == 1 else ALL, ALL, slice(0, ch))
-            if H == 1 or li == 0:
-                mm([(kl, ("idb", ALL), ("t1", ALL), True, False), (kl, ("idb", ALL), cols("t2", li * 192, 192), False, False)])
-            for s0, s1, how in cfg["pieces"][t][h]:
-                if s0 // 8 != li:
-                    continue
-                n = (s1 - s0) * lh
-                d_, r_ = cols("dd%d" % h, s0 * lh, n), cols("rr%d" % h, s0 * lh, n)
-                of, ff = cols("off%d" % h, (t * 16 + s0) * ch, (s1 - s0) * ch), ("fr", t * H + h, slice(0, n))
-                if how in "SB":
-                    gather("S", d_, pw, of, -1.0)
-                    dma("G", d_, ff, 2 * n, True)
-                else:
-                    gather("V", d_, pw, of, minus=ff)
-                ko = (kp, li, slice(s0 % 8, s0 % 8 + s1 - s0), slice(0, ch))
-
-                def pas(buf):
-                    mm([(ko, cols("wm", 15 - r, 128), cols(buf, s0 * lh + r, n // 16, 16), False, False) for r in range(16)])
-                if how in "AB":
-                    act(r_, d_, ACT.Abs)
-                else:
-                    pas(d_[0])
-                    ts(r_, d_, 0.0, -2.0, ALU.min, ALU.mult)
-                pas(r_[0])
-            if li:
-                for r in range(K):
-                    tt(("eq%d" % h, r), (m, 1, 2), cols("xp", h * 256 + r * ch, K * ch), ALU.is_equal)
-                for r0 in (0, 4):
-                    mm([((kp, 1, ALL, slice(0, ch)), ("big", ALL), ("eq%d" % h, r), False, False) for r in range(r0, r0 + 4)])
-            if H == 1 or li == 1:
-                mm([(kl, ("idb", ALL), ("t3", ALL), False, True)])
-
-        def sort8(li):
-            tag[0] = "s" + sfx
-            for q in (0, 1):
-                for ab in (0, 1):
-                    o = wires("SP"[q], [0, 1, 2, 3], li)
-                    tt(o[:3] + (sl(ab * ch, ch),), (kp, li, sl(4 * q, 4), slice(0, ch)), (m, li, ab, sl(4 * q, 4), ALL), ALU.add)
-            for big, o, a, b in NET8:
-                cx(big, o + (li,), ("S", a, li), ("P", b, li))
-
-        distances(0)
-        if split:
-            sort8(0)
-        distances(1)
-        if h == H - 1:
-            for t2 in ([t, t + 1] if t < R - 2 else []) if cfg["pp"] else ([t] if t < R - 1 else []):
-                renew(pw, t2)
-        sort8(1 if split else ALL)
+            how = cfg["slots"][t][h][li]
+            for kind, a0, n0 in runs([{"s": "f", "v": "f", "B": "S", "A": "V"}.get(c, c) for c in how]):
+                step = cfg["fold"] // 2 if kind == "f" else cfg["nc"][li] // 2 if t else 2
+                for a in range(a0, a0 + n0, step):
+                    n = min(step, a0 + n0 - a)
+                    s0, ns = li * K + 2 * a, 2 * n
+                    d_, r_ = cols(dd, s0 * LH, ns * LH), cols(rr, s0 * LH, ns * LH)
+                    if kind == "f":
+                        for e, b, m in runs(how[a:a + n]):
+                            gather(e.upper(), cols(dd, (s0 + 2 * b) * LH, 2 * m * LH), win, offsets(t, h, li, 2 * (a + b), 2 * m))
+                        w = 4 if ns % 4 == 0 else 2
+                        fold([((cols(dd, s * LH, w * LH), ("fr", t * H + h, slice(0, w * LH))), cols(rr, s * LH, w * LH))
+                              for s in range(s0, s0 + ns, w)], r_, 2, 2 * ns * LH)
+                        pas("wn", d_, s0, ns)
+                        pas("w2", r_, s0, ns)
+                        continue
+                    ff = ("fr", t * H + h, slice(0, ns * LH))
+                    if kind == "V":
+                        gather("V", d_, win, offsets(t, h, li, 2 * a, ns), minus=ff)
+                    else:
+                        gather("S", d_, win, offsets(t, h, li, 2 * a, ns), -1.0)
+                        dma("G", d_, ff, 2 * ns * LH, True)
+                    if folded:
+                        pas("w1", ff, s0, ns)
+                    for c, b, m in runs(how[a:a + n]):
+                        d_, r_ = cols(dd, (s0 + 2 * b) * LH, 2 * m * LH), cols(rr, (s0 + 2 * b) * LH, 2 * m * LH)
+                        if c in "AB":
+                            act(r_, d_, ACT.Abs)
+                        else:
+                            ts(r_, d_, 0.0, -2.0, ALU.min, ALU.mult)
+            for buf, kinds in ((dd, "SV"), (rr, "SVAB")):
+                for use, a, n in runs([c in kinds for c in how]):
+                    if use:
+                        pas("w1", cols(buf, (li * K + 2 * a) * LH, 2 * n * LH), li * K + 2 * a, 2 * n)
+        for r0 in (0, 4):
+            mm("k" + sfx, [((kp, 1, ALL, slice(0, CH)), ("big", ALL), ("eq%d" % h, r)) for r in range(r0, r0 + 4)])
+        if h == H - 1 and t < R - 2:
+            dma("Y", cols(win[0], 7 * L, L), cols("fc", t * L, L), 2 * L)
+        tag[0] = "s" + sfx
+        for q in (0, 1):
+            for ab in (0, 1):
+                o = wires("SP"[q], [0, 1, 2, 3], ALL)
+                tt(o[:3] + (sl(ab * CH, CH),), (kp, ALL, sl(4 * q, 4), slice(0, CH)), (pay, t, ALL, sl(4 * q, 4), sl(ab * CH, CH)), ALU.add)
+        marks["k" + sfx] = len(ops) - 1
+        loads("k" + sfx)
+        for big, o, a, b in NET8:
+            cx(big, o + (ALL,), ("S", a, ALL), ("P", b, ALL))
+        marks["n" + sfx] = len(ops) - 1
+        loads("n" + sfx)
         for c in MERGE:
             cx(*c)
-        lists(t + 1, h, ("fin%d" % h, ALL, slice(0, ch)), ("fin%d" % h, ALL, slice(ch, 2 * ch)), t == R - 1)
+        tmp = ("sp", 2 * h + 1, slice(4, 8), ALL)
+        ts((pay, t + 1, 0), ("fin%d" % h, ALL), 63, None, ALU.bitwise_and)
+        ts(tmp, (pay, t + 1, 0, ALL, slice(0, CH)), 64.0, None, ALU.mult)
+        tt((co, t + 1, 0), (pay, t + 1, 0, ALL, slice(CH, 2 * CH)), tmp, ALU.add)
+        cp(offsets(t + 1, h, 0), (co, t + 1, 0))
+        if t < R - 1:
+            send([(offsets(t + 1, h, 0), offsets(t + 1, h, 1))], 2 * K * CH)
+            hand_on(t + 1, h)
 
     def errors(t):
-        ga, bs = "ga%d" % t, "bs%d" % t
+        ga, bs, last = "ga%d" % t, "bs%d" % t, t == R - 1
         for q in range(4):
-            h, a, n = q * H // 4, q % (4 // H) * 2 * H, 2 * H
+            h, a = q // 2, q % 2 * 4
             tag[0] = "g%d%d" % (t, h)
             how = cfg["egather"][t][q]
-            for eng, a0, n0 in ([(how, a, n)] if how != "X" else [("V", a, n // 2), ("S", a + n // 2, n // 2)]):
-                gather(eng, (ga, h, sl(a0 * lh, n0 * lh)), "ew", cols("off%d" % h, ((t + 1) * 16 + a0) * ch, n0 * ch), -1.0)
-        nh = max(H, cfg["halves"][t])
-        n = L // nh
-        last, soft = t == R - 1, cfg["chain"][t] == "Q"
+            for eng, a0, n0 in ([(how.upper(), a, 4)] if how != "x" else [("V", a, 2), ("S", a + 2, 2)]):
+                gather(eng, (ga, h, sl(a0 * LH, n0 * LH)), cols("ew", t * L, W), offsets(t + 1, h, 0, a0, n0), -1.0)
+        parts = [(h, j * LH // len(s), LH // len(s), int(c)) for h, s in enumerate(cfg["chain"][t].split()) for j, c in enumerate(s)]
 
-        def bank(k, p):
-            if nh == 4:
-                return cols("bp%d" % p, 0, n) if p < 3 else ("kp1", 1, slice(0, 3), ALL)
-            if last and H == 2 and cfg["own"]:
-                return cols("bp%d" % (2 * p), 0, n) if k % 2 else (cols("bp1", 0, n) if p == 0 else ("kp1", 1, slice(0, 6), ALL))
-            if cfg.get("apart"):
-                return cols("bp%d" % (k % 2 if p == (t + cfg["apart"]) % 2 else 2), 0, n)
-            j = (nh * k + p) % (5 if last and H == 1 else 3)
-            if j == 3:
-                return ("kp0", 1, slice(0, n // 64), ALL)
-            return cols("bp%d" % j if j < 3 else "xp", 0, n)
+        def bank(p, k=K):
+            h, a, n, _ = parts[p]
+            if last:
+                return cols(("bp0", "bp1", "bp2", "xp")[2 * h + (k % 2 if n == LH else a // n)], 0, n)
+            return cols("bp%d" % ((2 * k + p) % 3), 0, n)
 
-        def gk(k, p):
-            return (ga, p * n // lh, sl(k * lh + p * n % lh, n))
+        def gk(k, p, buf=ga):
+            return (buf, parts[p][0], sl(k * LH + parts[p][1], parts[p][2]))
+        lim = (cols("mc", 1, 1), cols("mc", 0, 1), ALU.min, ALU.max)
         for k in range(K + 1):
-            for p in range(nh):
-                tag[0] = "e%d%d" % (t, p * n // lh)
-                u, s_ = bank(k, p), cols("uu", p * n, n)
+            for p, (h, a, n, skip) in enumerate(parts):
+                tag[0] = "e%d%d" % (t, h)
+                lanes, apart = sl(h * LH + a, n), K - skip
+                u, s_, grp = bank(p, k), ("uu", 0, lanes), "u%d%d%d" % (t, p, k)
+                terms = ([gk(k, p)] if k < K else []) + [s_] + [("uu", 1 + j - apart, lanes) for j in range(apart, k)]
                 if k == 0:
-                    ts(s_, gk(0, p), mcol(2), mcol(-2), ALU.min, ALU.max)
-                elif k < K:
-                    if cfg["chain"][t] == "H":
-                        mm([(u, ("hf", ALL), s_, True, True)], True)
-                        tt(u, gk(k, p), u, ALU.add)
-                    elif cfg["chain"][t] == "Z":
-                        act(u, s_, ACT.Copy, -0.5)
-                        tt(u, gk(k, p), u, ALU.add)
-                    else:
-                        mm([(u, ("idf", ALL), gk(k, p), True, False)], True)
-                        mm([(u, ("hf", ALL), s_, False, True)], True)
-                    if soft:
-                        act(cols("r1", p * n, n), u, ACT.Relu, -1.0, mcol(3 - k))
-                        act(u, cols("r1", p * n, n), ACT.Relu, -1.0, mcol(4))
-                    else:
-                        ts(u, u, mcol(2), mcol(-2), ALU.min, ALU.max)
+                    ts(s_, gk(0, p), *lim)
+                    continue
+                for j, term in enumerate(terms):
+                    mm(grp, [(u, ("hf" if j or k == K else "idf", ALL), term)], j == 0)
+                if k < apart:
+                    ts(u, u, *lim)
                     tt(s_, s_, u, ALU.add)
-                elif not soft:
-                    mm([(u, ("hf", ALL), s_, True, True)], True)
-                    if not last:
-                        tt(cols("ew", 8 * p * n + t + 1, n, 8), cols("xr", t * L + p * n, n), u, ALU.subtract)
-        b_ = (bs, ALL, slice(0, lh))
-        if soft:
-            act(b_, ("uu", ALL), ACT.Identity, -0.5, mcol(7))
-            tt(cols("ew", t + 1, L, 8), cols("xr", t * L, L), b_, ALU.subtract)
-        tag[0] = "p%d" % t
-        if last and H == 2:
+                elif k < K:
+                    ts(("uu", 1 + k - apart, lanes), u, *lim)
+                elif not last:
+                    tt(cols("ew", (7 + t) * L + h * LH + a, n), cols("xr", t * L + h * LH + a, n), u, ALU.subtract)
+        if last:
             for h in range(H):
                 tag[0] = "q%d" % h
                 sm, ng = ("kp%d" % h, 0, slice(0, 6), ALL), ("sp", 2 * h, slice(0, 8), ALL)
+                mine = [p for p in range(len(parts)) if parts[p][0] == h]
+                for j in range(2 if cfg["qadd"][h] == "D" else 1):
+                    for p in mine:
+                        act(gk(j, p, bs), bank(p), ACT.Copy)
+                dma("Y", cols("yb", t * L + h * LH, LH), (bs, h, slice(0, LH)), 768)
                 for k in range(K):
-                    for p in range(h * nh // 2, (h + 1) * nh // 2):
-                        tt(gk(k, p), gk(k, p), bank(K, p), ALU.add)
-                n = lh
-                act((bs, h), cols("uu", h * lh, lh), ACT.Copy, -0.5)
-                dma("Y", cols("yb", t * L + h * lh, lh), (bs, h), 768)
+                    if cfg["qadd"][h] == "V":
+                        for p in mine:
+                            tt(gk(k, p), gk(k, p), bank(p), ALU.add)
+                    elif k % 2 == 0:
+                        dma("G", (ga, h, sl(k * LH, 2 * LH)), (bs, h, slice(0, 2 * LH)), 1536, True)
                 for k in range(0, K, 2):
-                    g_ = (ga, h, sl(k * lh, 2 * lh))
-                    if k >= K - cfg["vabs"]:
+                    g_ = (ga, h, sl(k * LH, 2 * LH))
+                    if k >= K - cfg["vabs"][h]:
                         for j in (k, k + 1):
-                            gj = (ga, h, sl(j * lh, lh))
+                            gj = (ga, h, sl(j * LH, LH))
                             ts(ng, gj, -1.0, None, ALU.mult)
                             tt(gj, gj, ng, ALU.max)
                     else:
                         act(g_, g_, ACT.Abs)
                     act(g_, g_, ACT.Exp, -1.0)
                     for j in range(k, min(k + 2, K - 1)):
-                        mm([(sm, ("idf", ALL), (ga, h, sl(j * lh, lh)), j == 0, j == K - 2)], True)
-                tt(cols("so", h * lh, lh), (ga, h, sl((K - 1) * lh, lh)), sm, ALU.add)
-                n = L // nh
-                dma("Y", cols("ys", t * L + h * lh, lh), cols("so", h * lh, lh), 768)
+                        mm("q%d" % h, [(sm, ("idf", ALL), (ga, h, sl(j * LH, LH)))], j == 0)
+                tt(("so", t, sl(h * LH, LH)), (ga, h, sl((K - 1) * LH, LH)), sm, ALU.add)
+                dma("Y", cols("ys", t * L + h * LH, LH), ("so", t, sl(h * LH, LH)), 768)
             return
-        if last:
-            for k in range(K):
-                for p in range(nh):
-                    tt(gk(k, p), gk(k, p), bank(K, p), ALU.add)
-        if not soft:
-            act(b_, ("uu", ALL), ACT.Copy, -0.5)
+        tag[0] = "b%d" % t
+        for p in range(len(parts)):
+            for j in range({"D": 1, "F": 1, "E": 2, "C": 4}[cfg["padd"][t]]):
+                act(gk(j, p, bs), bank(p), ACT.Copy)
+
+    def spread(t):
+        ga, bs = "ga%d" % t, "bs%d" % t
+        tag[0] = "p%d" % t
+        copies = {"D": 1, "F": 1, "E": 2, "C": 4}[cfg["padd"][t]]
+        b_ = (bs, ALL, slice(0, LH))
         dma("Y", cols("yb", t * L, L), b_, 1536)
-        if not last:
-            dma("Y", (bs, ALL, sl(lh, lh)), b_, 1536)
-            dma("Y", (bs, ALL, sl(2 * lh, 2 * lh)), (bs, ALL, sl(0, 2 * lh)), 3072)
-            for q in range(2):
-                dma("G", (ga, ALL, sl(q * 4 * lh, 4 * lh)), (bs, ALL), 6144, True)
-            for q in range(4):
-                g_ = (ga, ALL, sl(q * 2 * lh, 2 * lh))
-                act(g_, g_, ACT.Abs)
-                act(g_, g_, ACT.Exp, -1.0)
-            for n2 in (4 * lh, 2 * lh, lh):
-                dma("G", (ga, ALL, sl(0, n2)), (ga, ALL, sl(n2, n2)), 4 * n2 * H, True)
-            dma("Y", cols("ys", t * L, L), (ga, ALL, sl(0, lh)), 1536)
+        if cfg["padd"][t] != "F":
+            while copies < cfg["bc"]:
+                dma("Y", (bs, ALL, sl(copies * LH, copies * LH)), (bs, ALL, sl(0, copies * LH)), 1536 * copies)
+                copies *= 2
+            if copies == 4:
+                for q in range(2):
+                    for h in range(H):
+                        dma("G", (ga, h, sl(q * 4 * LH, 4 * LH)), (bs, h), 3072, True)
+            else:
+                for q in range(4):
+                    dma("G", (ga, ALL, sl(q * 2 * LH, 2 * LH)), (bs, ALL, sl(0, 2 * LH)), 3072, True)
         else:
-            sm = ("kp0", 0, slice(0, 6), ALL) if H == 1 else ("kp0", ALL, slice(0, 6), ALL)
-            for k in range(K):
-                g_ = (ga, ALL, sl(k * lh, lh))
-                if k >= K - cfg["vabs"]:
-                    ng = ("sp", 0, slice(0, 8 * H), ALL) if H == 1 else ("sp", slice(0, 2), slice(0, 8), ALL)
-                    ts(ng, g_, -1.0, None, ALU.mult)
-                    tt(g_, g_, ng, ALU.max)
-                else:
-                    act(g_, g_, ACT.Abs)
-                act(g_, g_, ACT.Exp, -1.0)
-                if k < K - 1:
-                    mm([(sm, ("idf", ALL), g_, k == 0, k == K - 2)], True)
-            tt(("so", ALL), g_, sm, ALU.add)
-            dma("Y", cols("ys", t * L, L), ("so", ALL), 1536)
+            for h in range(H):
+                fold([(((ga, h, sl(k * LH, LH)), (bs, h, slice(0, LH))), (ga, h, sl(k * LH, LH))) for k in range(K)], (ga, h), 1, 4 * K * LH)
+        for q in range(4):
+            g_ = (ga, ALL, sl(q * 2 * LH, 2 * LH))
+            if t == R - 2 and q >= 4 - cfg["pabs"]:
+                for h in range(H):
+                    gh, ng = (ga, h, sl(q * 2 * LH, 2 * LH)), ("sp", slice(2, 4), slice(0, 8), ALL)
+                    ts(ng, gh, -1.0, None, ALU.mult)
+                    tt(gh, gh, ng, ALU.max)
+            else:
+                act(g_, g_, ACT.Abs)
+            act(g_, g_, ACT.Exp, -1.0)
+            if cfg["psum"][t] == "V" and q in (1, 2):
+                dma("G", (ga, ALL, sl(0, 2 * LH)), g_, 3072, True)
+        if cfg["psum"][t] == "V":
+            acc = ("sp", slice(1, 4, 2), slice(0, 8), ALL)
+            tt(acc, (ga, ALL, sl(6 * LH, LH)), (ga, ALL, sl(7 * LH, LH)), ALU.add)
+            tt(acc, (ga, ALL, sl(LH, LH)), acc, ALU.add)
+            tt(("so", t), (ga, ALL, sl(0, LH)), acc, ALU.add)
+            dma("Y", cols("ys", t * L, L), ("so", t), 1536)
+        elif cfg["psum"][t] == "D":
+            for n2 in (4 * LH, 2 * LH, LH):
+                dma("G", (ga, ALL, sl(0, n2)), (ga, ALL, sl(n2, n2)), 4 * n2 * H, True)
+            dma("Y", cols("ys", t * L, L), (ga, ALL, sl(0, LH)), 1536)
+        elif cfg["psum"][t] == "P":
+            sm = ("kp0", ALL, slice(0, 6), ALL)
+            mm("p", [(sm, ("idf", ALL), (ga, ALL, sl(0, LH)))], True)
+            for k in range(1, K):
+                for h in range(H):
+                    mm("p", [(("kp0", h, slice(0, 6), ALL), ("idf", ALL), (ga, h, sl(k * LH, LH)))])
+            act(("so", t), sm, ACT.Copy)
+            dma("Y", cols("ys", t * L, L), ("so", t), 1536)
+        else:
+            fold([([(ga, h, sl(k * LH, LH)) for k in range(K)], ("so", t, sl(h * LH, LH))) for h in range(H)], ("so", t), 1, 4 * L)
+            dma("Y", cols("ys", t * L, L), ("so", t), 1536)
 
     for t in range(R):
         for h in range(H):
-            select(t, h)
+            choice(t, h)
+        for t2 in range(t):
+            if t == (t2 + 1 if cfg["psum"][t2] in "DF" else R - 1):
+                spread(t2)
         errors(t)
     return ops
 
 
 def analyse(cfg):
     ops = build_ops(cfg)
-    SC = scratch(cfg["H"])
+    SC = scratch(cfg)
     index = {b: np.arange(int(np.prod(v[1][1:]))).reshape(v[1][1:]) for b, v in SC.items()}
     lastw = {b: np.full(index[b].size, -1) for b in SC}
     readers = {b: [] for b in SC}
+    adders = {b: [] for b in SC}
     bank = {}
-    deps = []
+    deps, fed = [], []
+
+    def mask(a):
+        m = np.zeros(index[a[0]].size, bool)
+        m[index[a[0]][a[1:]].ravel()] = True
+        return m
+
+    def meet(users, m):
+        return [j for j, mj in users if np.any(mj & m)]
+
     for i, o in enumerate(ops):
+        raw = set([o["after"]] if "after" in o else [])
         d = set()
-        if "after" in o:
-            d.add(o["after"])
         for a in o["rd"]:
-            e = index[a[0]][a[1:]].ravel()
-            d.update(int(v) for v in np.unique(lastw[a[0]][e]))
+            m = mask(a)
+            raw.update(int(v) for v in np.unique(lastw[a[0]][m]))
+            raw.update(meet(adders[a[0]], m))
+        for a in o["acc"] + o["wr"]:
+            m = mask(a)
+            d.update(int(v) for v in np.unique(lastw[a[0]][m]))
+            d.update(meet(readers[a[0]], m))
         for a in o["wr"]:
-            e = index[a[0]][a[1:]].ravel()
-            d.update(int(v) for v in np.unique(lastw[a[0]][e]))
-            mask = np.zeros(index[a[0]].size, bool)
-            mask[e] = True
-            keep = []
-            for j, m in readers[a[0]]:
-                if np.any(m & mask):
-                    d.add(j)
-                if np.any(m & ~mask):
-                    keep.append((j, m & ~mask))
-            readers[a[0]] = keep
+            m = mask(a)
+            d.update(meet(adders[a[0]], m))
+            for users in (readers, adders):
+                users[a[0]] = [(j, mj & ~m) for j, mj in users[a[0]] if np.any(mj & ~m)]
         touched = set()
-        for a in o["rd"] + o["wr"]:
+        for a in o["rd"] + o["wr"] + o["acc"]:
             if SC[a[0]][0] == "psum":
                 touched.update((a[0], int(v)) for v in np.unique(index[a[0]][a[1:]] // 512))
         for b in touched:
@@ -485,83 +560,163 @@ def analyse(cfg):
                 js, before = [], js
             d.update(before)
             bank[b] = (o["eng"], js + [i], before)
-        for a in o["rd"]:
-            mask = np.zeros(index[a[0]].size, bool)
-            mask[index[a[0]][a[1:]].ravel()] = True
-            readers[a[0]].append((i, mask))
+        for a in o["rd"] if o["kind"] != "fold" else []:
+            readers[a[0]].append((i, mask(a)))
+        for a in o["acc"]:
+            adders[a[0]].append((i, mask(a)))
         for a in o["wr"]:
             lastw[a[0]][index[a[0]][a[1:]].ravel()] = i
-        d.discard(-1)
-        d.discard(i)
-        deps.append(sorted(d))
-    return ops, deps
+        d = (d | raw) - {-1, i}
+        known = 0
+        for j in d:
+            known |= fed[j]
+        d = {j for j in d if not known >> j & 1 or j == o.get("after")}
+        for j in d:
+            known |= 1 << j
+        deps.append(sorted((d | {o.get("behind")}) - {None}))
+        fed.append(0 if o["kind"] == "recv" and ops[o["after"]]["kind"] == "send" else known)
+    return ops, deps, fed
 
 
-def make_plan(cfg, known=None):
-    ops, deps = known or analyse(cfg)
+def times(ops, c):
+    out = []
+    for o in ops:
+        e, k, n = o["eng"], o["kind"], o["work"]
+        if k == "g":
+            out.append(((50 if e == "V" else 65) + c["cy"] * c["ga"] * n, 0.0, 0.0))
+        elif k == "c":
+            fix = {"V": c["ov"], "S": 65.0, "P": 0.0, "G": 170.0}[e]
+            out.append((fix + c["cy"] * max(n, c["mn"] if e == "V" else 0), 0.0, 60.0 if e == "P" else 0.0))
+        elif k == "dma":
+            out.append((c["dg"] if e == "G" else 80.0, n / c["db"] + o["rows"] * c["row"], c["dl"]))
+        elif k == "send":
+            far = (64 if len(o["pairs"]) > 2 else 16 * len(o["pairs"])) * c["far"]
+            out.append((c["rg"], n / c["db"] + far / 2, c["rl"] + n / c["rb"] + far / 2))
+        elif k == "fold":
+            out.append((c["rg"], len(o["pairs"][0][0]) * n / c["db"], c["fl"] + n / c["fb"]))
+        else:
+            out.append((0.0, 0.0, 0.0))
+    return out
+
+
+def graph(ops, before, after, soft, c, back=False):
+    tm = times(ops, c)
+    eng = [o["eng"] for o in ops]
+    edges = []
+    for i in range(len(ops)):
+        row = []
+        for j in after[i]:
+            if eng[i] == eng[j] and ((i, j) in soft or (j, i) in soft):
+                v = -sum(tm[j][1:]) if back else -sum(tm[i][1:])
+            elif eng[i] is None or eng[j] is None:
+                v = c["hop"] if (eng[i] is None) != back else 0.0
+            else:
+                v = c["same"] if eng[i] == eng[j] else c["hop"]
+            row.append((j, v + (tm[j][1] + tm[j][2] if back else 0.0)))
+        edges.append(row)
+    if back:
+        return [(t[0], 0.0, 0.0) for t in tm], eng, edges, [len(d) for d in before], [t[1] + t[2] for t in tm]
+    return tm, eng, edges, [len(d) for d in before], [0.0] * len(ops)
+
+
+def run(gr, prio=None, order=None, look={}):
+    tm, eng, edges, left, ready = gr
+    n = len(eng)
+    left, ready = list(left), list(ready)
+    done, start = [0.0] * n, [0.0] * n
+    free = {e: 0.0 for e in "VSPGY"}
+    out = {e: [] for e in "VSPGY"}
+    pool = {e: [i for i in range(n) if eng[i] == e and not left[i]] for e in "VSPGY"}
+    head = {e: order[e][0] for e in order} if order else None
+    dmas = 0.0
+    while True:
+        t0, e = 1e30, None
+        for q in "VSPGY":
+            if order:
+                i = head[q]
+                if i is None or left[i]:
+                    continue
+                v = ready[i]
+            elif pool[q]:
+                v = min([ready[j] for j in pool[q]])
+            else:
+                continue
+            if v < free[q]:
+                v = free[q]
+            if v < t0:
+                t0, e = v, q
+        if e is None:
+            return out, start, done
+        if order:
+            i = head[e]
+            p = len(out[e]) + 1
+            head[e] = order[e][p] if p < len(order[e]) else None
+        else:
+            t1 = t0 + look.get(e, 0.0)
+            i = -max([(prio[j], -j) for j in pool[e] if ready[j] <= t1])[1]
+            pool[e].remove(i)
+            t0 = max(t0, ready[i])
+        start[i] = t0
+        t = free[e] = t0 + tm[i][0]
+        out[e].append(i)
+        if tm[i][1]:
+            t = dmas = max(dmas, t) + tm[i][1]
+        todo = [(i, t + tm[i][2])]
+        while todo:
+            i, t = todo.pop()
+            done[i] = t
+            for j, v in edges[i]:
+                if t + v > ready[j]:
+                    ready[j] = t + v
+                left[j] -= 1
+                if not left[j]:
+                    if eng[j] is None:
+                        todo.append((j, ready[j]))
+                    elif not order:
+                        pool[eng[j]].append(j)
+
+
+def plan_order(cfg, known, costs, judges):
+    ops, deps, fed = known
     n = len(ops)
     succ = [[] for _ in range(n)]
+    soft = set()
     for i in range(n):
         for j in deps[i]:
             succ[j].append(i)
-    prio = [0.0] * n
+            if ops[i]["eng"] == ops[j]["eng"] == "P" or ops[i].get("behind") == j:
+                soft.add((j, i))
+    ahead, back = graph(ops, deps, succ, soft, costs), graph(ops, succ, deps, soft, costs, True)
+    views = [(graph(ops, deps, succ, soft, c), c["cy"]) for c in judges]
+
+    def judge(order):
+        return sum(max(run(g, order=order)[2]) / cy for g, cy in views)
+    tm = times(ops, costs)
+    path = [0.0] * n
     for i in range(n - 1, -1, -1):
-        prio[i] = ops[i]["cost"] + ops[i]["lat"] + max([prio[j] + HOP for j in succ[i]] + [0.0])
-    for i in range(n):
-        prio[i] += cfg["bias"].get(ops[i]["tag"], 0.0) * 1000
-    eng = [o["eng"] for o in ops]
-    cost = [o["cost"] for o in ops]
-    lat = [o["lat"] for o in ops]
-
-    def run(prio, before, after, back):
-        left = [len(d) for d in before]
-        ready_at = [lat[i] if back else 0.0 for i in range(n)]
-        done = [0.0] * n
-        free = {e: 0.0 for e in "VSPGY"}
-        order = {e: [] for e in "VSPGY"}
-        start = [0.0] * n
-        pool = {e: [] for e in "VSPGY"}
-
-        def finish(i, t):
-            done[i] = t
-            for j in after[i]:
-                if eng[i] == eng[j] == "P":
-                    v = t if back else t - lat[i]
-                else:
-                    v = t + HOP + (lat[j] if back else 0.0)
-                if v > ready_at[j]:
-                    ready_at[j] = v
-                left[j] -= 1
-                if left[j] == 0:
-                    if eng[j] is None:
-                        finish(j, ready_at[j])
-                    else:
-                        pool[eng[j]].append(j)
-        for i in range(n):
-            if not before[i]:
-                pool[eng[i]].append(i)
-        while True:
-            t0, e = min([(max(free[e], min([ready_at[j] for j in pool[e]])), e) for e in pool if pool[e]] + [(1e30, "")])
-            if not e:
-                return order, start, done
-            i = max([(prio[j], -j) for j in pool[e] if ready_at[j] <= t0 + cfg["look"]])
-            i = -i[1]
-            pool[e].remove(i)
-            start[i] = max(ready_at[i], free[e])
-            free[e] = start[i] + cost[i]
-            order[e].append(i)
-            finish(i, free[e] + (0.0 if back else lat[i]))
-
-    order, start, done = run(prio, deps, succ, False)
-    last = done
+        path[i] = sum(tm[i]) + max([path[j] + costs["same"] for j in succ[i]] + [0.0])
+    kinds = sorted(set(o["tag"] + str(o["eng"]) for o in ops))
+    kind = [kinds.index(o["tag"] + str(o["eng"])) for o in ops]
     rs = np.random.RandomState(cfg.get("seed", 0))
-    for _ in range(cfg.get("turns", 0)):
-        _, _, bd = run(last, succ, deps, True)
-        if cfg.get("seed"):
-            bd = [float(v) for v in np.array(bd) + cfg["noise"] * rs.rand(n)]
-        o2, s2, last = run(bd, deps, succ, False)
-        if max(last) < max(done):
-            order, start, done = o2, s2, last
+    kind = np.array(kind)
+    order, _, done = run(ahead, prio=path)
+    best = (judge(order), order, done, np.array(path))
+    for turn in range(cfg["tries"]):
+        if turn < 3 or turn % 40 == 0:
+            prio = np.array(run(back, prio=done if turn < 3 else best[2])[2])
+        else:
+            prio = best[3] + ((rs.rand(len(kinds)) < cfg["share"]) * rs.randn(len(kinds)) * cfg["move"])[kind]
+        order, _, done = run(ahead, prio=prio.tolist(), look=cfg["look"])
+        v = judge(order)
+        if v <= best[0]:
+            best = (v, order, done, prio)
+    return best[1], soft, succ
+
+
+def make_plan(cfg):
+    known = analyse(cfg)
+    ops, deps, _ = known
+    order, soft, _ = plan_order(cfg, known, COSTS, JUDGES)
     pos = {}
     for e in order:
         for p, i in enumerate(order[e]):
@@ -573,13 +728,9 @@ def make_plan(cfg, known=None):
         for i in order[e]:
             w = {}
             for j in deps[i]:
-                oj = ops[j]
-                if oj["kind"] == "c":
-                    if oj["eng"] == e == "P":
-                        continue
-                    key, val = oj["eng"], pos[j]
-                else:
-                    key, val = j, 0
+                if (j, i) in soft:
+                    continue
+                key, val = (ops[j]["eng"], pos[j]) if ops[j]["kind"] in "cg" else (j, 0)
                 if seen.get(key, -1) < val:
                     w[key] = max(w.get(key, -1), val)
             seen.update(w)
@@ -590,52 +741,98 @@ def make_plan(cfg, known=None):
     for e in order:
         c = 0
         for i in order[e]:
-            if ops[i]["kind"] == "c" and i in needed:
+            if ops[i]["kind"] in "cg" and i in needed:
                 c += 1
                 count[i] = c
     sems = {}
     for i, o in enumerate(ops):
-        if o["kind"] != "c":
+        if o["kind"] in ("dma", "recv"):
             sems[i] = "d%d" % len(sems)
-    return {"ops": ops, "order": order, "waits": waits, "needed": needed, "count": count, "sems": sems,
-            "start": start, "done": done}
+    closes = {ops[i]["group"]: i for i in order["P"]}
+    return {"ops": ops, "order": order, "waits": waits, "needed": needed, "count": count, "sems": sems, "closes": set(closes.values())}
+
+
+def helpers(T, topo):
+    out = {}
+    for c in T.cores:
+        out[c] = [k for k in topo.cores_of(c) if T.rank_of(k) is None and topo.die(k) == topo.die(c) and k not in out.values()][0]
+    return out
+
+
+def shares(engines, n):
+    size = [len(engines)]
+    while len(size) < n:
+        size.sort()
+        size = size[:-1] + [size[-1] // 2] * 2
+    size.sort(reverse=True)
+    return [sum(1 << e for e in engines[sum(size[:j]):sum(size[:j + 1])]) for j in range(n)]
 
 
 def rank_program(g, core, T, topo):
-    rank = T.rank_of(core)
-    if rank is None:
-        return
     if "p" not in PLAN:
         PLAN["p"] = make_plan(CFG)
     p = PLAN["p"]
     ops, order, sems = p["ops"], p["order"], p["sems"]
-    dst = T.cores[(rank + 1) % len(T.cores)]
-    assert topo.may_write(core, dst)
-    rid, pid, _ = topo.addr(dst)
-    ne = 8
-    mask = sum(1 << e for e in topo.engines(core, dst)[:ne])
-    x = {"V": g.vector, "S": g.scalar, "P": g.tensor, "G": g, "Y": g.sync, "ap": lambda a: T[a[0]][(ALL,) + a[1:]]}
+    helper = helpers(T, topo)
     recv_of = {o["after"]: j for j, o in enumerate(ops) if o["kind"] == "recv"}
+
+    def ap(a):
+        return T[a[0]][(ALL,) + a[1:]]
+
+    rank = T.rank_of(core)
+    if rank is None:
+        for home in [c for c in helper if helper[c] == core]:
+            rid, pid, _ = topo.addr(home)
+            n, sent = len(topo.engines(core, home)), 0
+            for i in order["G"]:
+                if ops[i]["kind"] == "fold":
+                    s = T.sem[sems[recv_of[i]]]
+                    g.wait_ge(s, n)
+                    g.remote_dma(ap(ops[i]["back"]), ap(ops[i]["back"]), s, T.sem.out, pid, rid, topo.mask(core, home))
+                    sent += n
+            if sent:
+                g.wait_ge(T.sem.out, sent)
+        return
+    nxt = T.cores[(rank + 1) % len(T.cores)]
+    assert topo.may_write(core, nxt)
+    ne = min(len(topo.engines(a, b)) for a, b in zip(T.cores, T.cores[1:] + T.cores[:1]))
+    way = {"send": (nxt, topo.engines(core, nxt)[:ne]), "fold": (helper[core], topo.engines(core, helper[core]))}
+    x = {"V": g.vector, "S": g.scalar, "P": g.tensor, "G": g, "Y": g.sync, "ap": ap}
     for e in "YGVSP":
         q = x[e]
-        late = []
+        late, sent = [], 0
         for i in order[e]:
             o = ops[i]
             for key, val in p["waits"][i].items():
                 if key in order:
                     q.wait_ge(T.sem["c" + key], p["count"][order[key][val]])
                 else:
-                    q.wait_ge(T.sem[sems[key]], ne if ops[key]["kind"] == "recv" else 16)
-            if o["kind"] == "send":
-                g.remote_dma(x["ap"](o["dst"]), x["ap"](o["src"]), T.sem[sems[recv_of[i]]], T.sem[sems[i]], pid, rid, mask)
-                late.append((sems[i], ne))
+                    q.wait_ge(T.sem[sems[key]], len(way[ops[ops[key]["after"]]["kind"]][1]) if ops[key]["kind"] == "recv" else 16)
+            if o["kind"] in way:
+                dst, engines = way[o["kind"]]
+                rid, pid, _ = topo.addr(dst)
+                masks = shares(engines, len(o["pairs"]))
+                s = T.sem[sems[recv_of[i]]]
+                if o["kind"] == "fold":
+                    g.remote_dma_fused([RemoteDMATransfer(dst_ids=[DstId(rid=rid, pnc=pid)], dma_engine_mask=m, remote_sem=s,
+                                                          srcs=[ap(a) for a in srcs], dsts=[ap(d)], alu_op=o["alu"])
+                                        for (srcs, d), m in zip(o["pairs"], masks)], local_sem=T.sem.out)
+                elif len(masks) > 1:
+                    g.remote_dma_fused([RemoteDMATransfer(dst_ids=[DstId(rid=rid, pnc=pid)], dma_engine_mask=m, remote_sem=s,
+                                                          src=ap(a), dst=ap(d)) for (a, d), m in zip(o["pairs"], masks)], local_sem=T.sem.out)
+                else:
+                    g.remote_dma(ap(o["pairs"][0][1]), ap(o["pairs"][0][0]), s, T.sem.out, pid, rid, masks[0])
+                sent += len(engines)
             elif o["kind"] == "dma":
                 o["emit"](x).then_inc(T.sem[sems[i]], 16)
                 if i not in p["needed"]:
-                    late.append((sems[i], 16))
+                    late.append(sems[i])
             else:
+                x["stop"] = i in p["closes"]
                 ins = o["emit"](x)
                 if i in p["needed"]:
                     ins.then_inc(T.sem["c" + e], 1)
         for s in late:
-            q.wait_ge(T.sem[s[0]], s[1])
+            q.wait_ge(T.sem[s], 16)
+        if sent:
+            q.wait_ge(T.sem.out, sent)

import numpy as np
from concourse.bass import DstId, RemoteDMATransfer
from concourse.mybir import AluOpType as ALU, ActivationFunctionType as ACT

L, K, R, W, C = 384, 8, 4, 3072, 24
H = 2
CH, LH = C // H, L // H

CFG = {
    "slots": [[("AAAA", "VVVV"), ("SSBB", "BBBB")]] + [[("BBSS", "SSSS")] * 2] * 3,
    "fold": 8,
    "egather": ["ssss", "ssss", "ssss", "ssxx"],
    "chain": ["0 0", "0 0", "0 0", "0 00"], "qadd": "VV",
    "padd": "EEE", "psum": "DDV", "bc": 2, "co": "V", "nc": [4, 4], "run": 8,
    "prel": "VVVVVSSS", "erel": "SSSSSSSS",
    "vabs": [0, 2], "pabs": 0, "tries": 3500, "look": {"G": 600.0}, "share": 0.04, "move": 4000.0,
    "gates": {"e": "m1", "p": "k00", "1": "k00", "x": "k01", "2": "k10", "3": "k20"},
}


def scratch(cfg):
    s = {
        "ndl": ("sbuf", [128, K, C], "int32"), "tb": ("sbuf", [128, K, C], "int32"), "tj": ("sbuf", [128, K, C], "int32"),
        "tq": ("sbuf", [128, K, C], "int32"),
        "praw": ("sbuf", [128, L, 8], "bfloat16"), "eraw": ("sbuf", [128, L, 8], "bfloat16"),
        "pw0": ("sbuf", [128, 10 * L], "bfloat16"), "pw1": ("sbuf", [128, 10 * L], "bfloat16"), "ew": ("sbuf", [128, 11 * L], "float32"),
        "fr": ("sbuf", [128, R * H, K * LH], "bfloat16"), "xr": ("sbuf", [128, R * L], "bfloat16"),
        "dls": ("sbuf", [128, 1], "float32"), "mc": ("sbuf", [128, 2], "float32"),
        "uu": ("sbuf", [128, 4, L], "float32"), "so": ("sbuf", [128, R, L], "float32"),
        "w1": ("sbuf", [128, 144], "bfloat16"), "w2": ("sbuf", [128, 144], "bfloat16"), "wn": ("sbuf", [128, 144], "bfloat16"),
        "wt": ("sbuf", [128, 8], "bfloat16"),
        "onesf": ("sbuf", [128, 128], "float32"), "idf": ("sbuf", [128, 128], "float32"), "hf": ("sbuf", [128, 128], "float32"),
        "nf": ("sbuf", [128, 128], "float32"), "idb": ("sbuf", [128, 128], "bfloat16"), "big": ("sbuf", [128, 128], "bfloat16"),
        "t2": ("sbuf", [128, 16 * CH], "bfloat16"),
    }
    for t in range(R):
        s["ga%d" % t] = ("sbuf", [128, H, K * LH], "float32")
        s["bs%d" % t] = ("sbuf", [128, H, (4 if t < R - 1 else 2) * LH], "float32")
    for h in range(H):
        s["off%d" % h] = ("sbuf", [128, 5 * 16 * CH], "uint16")
        s["pay%d" % h] = ("sbuf", [128, R + 1, 2, K, 2 * CH], "int32")
        s["co%d" % h] = ("sbuf", [128, R + 1, 2, K * CH], "float32")
        s["dd%d" % h] = ("sbuf", [128, 16 * LH], "bfloat16")
        s["rr%d" % h] = ("sbuf", [128, 16 * LH], "bfloat16")
        s["eq%d" % h] = ("sbuf", [128, K, K * CH], "bfloat16")
        s["ss%d" % h] = ("sbuf", [128, 2, 17, 2 * CH], "float32")
        s["fin%d" % h] = ("sbuf", [128, K, 2 * CH], "int32")
    for h in range(H):
        s["kp%d" % h] = ("psum", [128, 2, K, 32], "float32")
    for b in ("xp", "bp0", "bp1", "bp2"):
        s[b] = ("psum", [128, 512], "float32")
    s["sp"] = ("psum", [128, 2 * H, 10, 2 * CH], "float32")
    return s


SCRATCH = scratch(CFG)
SEMAPHORES = ["cV", "cS", "cP", "cG", "out"] + ["d%d" % i for i in range(144)]

COSTS = {"cy": 1.0, "ga": 1.7, "ov": 45.0, "mn": 50, "hop": 150.0, "same": 100.0,
         "dg": 700.0, "dl": 1800.0, "db": 650.0, "rg": 900.0, "rl": 2000.0, "rb": 120.0, "fl": 4400.0, "fb": 400.0, "row": 12.0, "far": 30.0}
JUDGES = [dict(COSTS, cy=0.83, ga=1.56), dict(COSTS, cy=1.1, ga=1.2), dict(COSTS, cy=1.15, ga=2.05, rg=1200.0, dl=2100.0),
          dict(COSTS, cy=0.95, dg=1000.0, rg=1500.0, dl=2100.0, rl=2800.0, db=600.0, row=20.0, far=60.0)]
ALL = slice(None)
PLAN = {}
NET8 = [
    (0, ("S", [4, 6]), [0, 2], [0, 2]), (1, ("S", [5, 7]), [0, 2], [0, 2]),
    (0, ("P", [4, 6]), [1, 3], [1, 3]), (1, ("P", [5, 7]), [1, 3], [1, 3]),
    (0, ("S", [8, 12]), [4, 5], [4, 5]), (1, ("P", [0, 8]), [4, 5], [4, 5]),
    (0, ("P", [2, 3]), [6, 7], [6, 7]), (1, ("S", [0, 11]), [6, 7], [6, 7]),
    (0, ("S", [9]), [12], [0]), (1, ("S", [10]), [12], [0]),
    (0, ("P", [4]), [0], [3]), (1, ("P", [6]), [0], [3]),
    (0, ("S", [0, 1, 2, 3]), [8, 9, 10, 11], [2, 4, 6, 8]), (1, ("P", [3, 5, 7, 9]), [8, 9, 10, 11], [2, 4, 6, 8]),
    (0, ("P", [1, 2]), [2, 3], [3, 5]), (1, ("S", [5, 6]), [2, 3], [3, 5]),
    (1, ("S", [8]), [1], [1]), (0, ("S", [4, 12]), [1, 5], [1, 2]),
    (0, ("P", [3]), [6], [7]), (1, ("P", [0, 6]), [5, 6], [2, 7]),
]
MERGE = [
    (0, ("S", [13, 14, 15, 16], 0), ("S", [0, 4, 8, 12], 0), ("P", [9, 6, 3, 0], 1)),
    (0, ("P", [0, 1, 2, 3], 1), ("S", [12, 8, 4, 0], 1), ("P", [0, 3, 6, 9], 0)),
    (1, ("S", [0, 1], 0), ("S", [13, 14], 0), ("P", [0, 1], 1)), (1, ("P", [0, 1], 0), ("S", [15, 16], 0), ("P", [2, 3], 1)),
    (0, ("S", [2, 3], 0), ("S", [13, 14], 0), ("P", [0, 1], 1)), (0, ("P", [2, 3], 0), ("S", [15, 16], 0), ("P", [2, 3], 1)),
    (1, ("S", [4, 6], 0), ("S", [0, 2], 0), ("P", [0, 2], 0)), (1, ("P", [4, 6], 0), ("S", [1, 3], 0), ("P", [1, 3], 0)),
    (0, ("S", [5, 7], 0), ("S", [0, 2], 0), ("P", [0, 2], 0)), (0, ("P", [5, 7], 0), ("S", [1, 3], 0), ("P", [1, 3], 0)),
    (1, ("F", [0, 2, 4, 6], 0), ("S", [4, 5, 6, 7], 0), ("P", [4, 5, 6, 7], 0)),
    (0, ("F", [1, 3, 5, 7], 0), ("S", [4, 5, 6, 7], 0), ("P", [4, 5, 6, 7], 0)),
]


def sl(a, n, st=1):
    e = a + st * (n - 1) + (1 if st > 0 else -1)
    return slice(a, e if e >= 0 else None, st)


def runs(s):
    out = []
    for i, c in enumerate(s):
        if out and out[-1][0] == c:
            out[-1][2] += 1
        else:
            out.append([c, i, 1])
    return out


def build_ops(cfg):
    ops = []
    tag = ["i"]
    marks = {}
    SC = scratch(cfg)

    def op(eng, emit, rd, wr, work, kind="c", acc=(), **more):
        ops.append(dict(more, tag=tag[0], eng=eng, emit=emit, rd=list(rd), wr=list(wr), acc=list(acc), work=work, kind=kind))
        return len(ops) - 1

    def size(a):
        n = 1
        for j, d in enumerate(SC[a[0]][1][1:]):
            if j + 1 >= len(a):
                n *= d
            elif isinstance(a[j + 1], slice):
                n *= len(range(*a[j + 1].indices(d)))
        return n

    def rows(a):
        if a[0] not in SC:
            return 1
        e = np.arange(int(np.prod(SC[a[0]][1][1:]))).reshape(SC[a[0]][1][1:])[a[1:]].ravel()
        return 1 + int(np.sum(np.diff(e) != 1))

    def psum(a):
        return SC[a[0]][0] == "psum"

    def two(a):
        return SC[a[0]][2] in ("bfloat16", "uint16")

    def tt(o, a, b, alu):
        n = size(o) * (1 if psum(a) or psum(b) else 2)
        op("V", lambda x: x["V"].tensor_tensor(x["ap"](o), x["ap"](a), x["ap"](b), alu), [a, b], [o], n)

    def ts(o, a, s1, s2, o0, o1=None):
        n = size(o) * (0.5 if two(o) and two(a) else 1)
        cs = [s for s in (s1, s2) if isinstance(s, tuple)]

        def emit(x):
            v1 = x["ap"](s1) if isinstance(s1, tuple) else s1
            v2 = x["ap"](s2) if isinstance(s2, tuple) else s2
            if o1 is None:
                return x["V"].tensor_scalar(x["ap"](o), x["ap"](a), v1, None, o0)
            return x["V"].tensor_scalar(x["ap"](o), x["ap"](a), v1, v2, o0, o1)
        op("V", emit, [a] + cs, [o], n)

    def cp(o, a):
        op("V", lambda x: x["V"].tensor_copy(x["ap"](o), x["ap"](a)), [a], [o], size(o) * (0.5 if two(o) and two(a) else 1))

    def fill(o, v):
        op("V", lambda x: x["V"].memset(x["ap"](o), v), [], [o], size(o) * (0.5 if two(o) else 1))

    def act(o, a, f, scale=1.0):
        op("S", lambda x: x["S"].activation(x["ap"](o), x["ap"](a), f, scale=scale), [a], [o], size(o))

    def select(o, a, pattern, cmp, base, mult):
        op("G", lambda x: x["G"].affine_select(x["ap"](o), x["ap"](a), pattern, cmp, 0.0, base, mult), [a], [o], 2 * size(o))

    def move(eng, o, a):
        if eng == "V":
            cp(o, a)
        elif eng == "S":
            act(o, a, ACT.Copy)
        else:
            select(o, a, [[0, size(o)]], ALU.is_ge, 0, 0)

    def gather(eng, o, wa, of, scale=1.0, minus=None):
        if eng == "S":
            op("S", lambda x: x["S"].activation(x["ap"](o), x["ap"](wa).indirect(x["ap"](of)), ACT.Copy, scale=scale),
               [wa, of], [o], size(o), "g")
        elif minus is None:
            op("V", lambda x: x["V"].tensor_scalar(x["ap"](o), x["ap"](wa).indirect(x["ap"](of)), scale, None, ALU.mult),
               [wa, of], [o], size(o), "g")
        else:
            op("V", lambda x: x["V"].tensor_tensor(x["ap"](o), x["ap"](wa).indirect(x["ap"](of)), x["ap"](minus), ALU.subtract),
               [wa, of, minus], [o], size(o), "g")

    def mm(group, items, start=False):
        def emit(x):
            for j, (o, w, r) in enumerate(items):
                last = x["P"].matmul(x["ap"](o), x["ap"](w), x["ap"](r), start and j == 0, x["stop"] and j == len(items) - 1)
            return last
        n = sum(max(64, size(it[2])) * (0.5 if two(it[2]) else 2) for it in items)
        outs = [it[0] for it in items]
        op("P", emit, [it[1] for it in items] + [it[2] for it in items], outs[:1] if start else [], n,
           acc=outs[1:] if start else outs, group=group)

    def dma(eng, o, a, nbytes, add=False, gate=None):
        def emit(x):
            if add:
                return x["G"].dma_start(x["ap"](o), x["ap"](a), accum_op=ALU.add)
            return x[eng].dma_start(x["ap"](o), x["ap"](a))
        op(eng, emit, ([a] if a[0] in SC else []) + ([o] if add else []), [o] if o[0] in SC else [],
           nbytes * 128 * (2 if add else 1), "dma", rows=8 * max(rows(o), rows(a)), **({} if gate is None else {"after": gate}))

    def send(pairs, nbytes):
        i = op("G", None, [p[0] for p in pairs], [], nbytes * 128, "send", pairs=pairs, behind=marks.get("sent"))
        marks["sent"] = i
        op(None, None, [], [p[1] for p in pairs], 0, "recv", after=i)

    def fold(pairs, back, alu, nbytes):
        srcs = [s for p in pairs for s in p[0]]
        i = op("G", None, srcs, [], nbytes * 128, "fold", pairs=pairs, alu=alu, back=back)
        op(None, None, srcs, [back], 0, "recv", after=i)

    def cols(b, a, n, st=1):
        return (b, sl(a, n, st))

    dma("Y", ("ndl", ALL), ("nd", ALL), 768)
    dma("Y", ("praw", ALL), ("pa", ALL), 6144)
    for q in range(4):
        dma("Y", ("fr", slice(0, H), sl(q * LH, LH)), cols("fc", 0, L), 768)
    fill(("onesf", ALL), 1.0)
    fill(("w1", ALL), 0.0)
    fill(("wt", ALL), 1024.0)
    select(("wt", ALL), ("wt", ALL), [[-16, 8]], ALU.is_ge, 0, 1)
    select(cols("w1", 15, 8, 16), ("wt", ALL), [[16, 8]], ALU.is_ge, 15, -1)
    select(("idf", ALL), ("onesf", ALL), [[-1, 128]], ALU.is_equal, 0, 1)
    op("G", lambda x: x["G"].iota(x["ap"](("t2", ALL)), [[64, 16], [0, CH]], 0, 0, allow_small_or_imprecise_dtypes=True),
       [], [("t2", ALL)], 32 * CH)
    if any(c in "sv" for day in cfg["slots"] for half in day for s in half for c in s):
        act(("w2", ALL), ("w1", ALL), ACT.Copy, 2.0)
        act(("wn", ALL), ("w1", ALL), ACT.Copy, -1.0)
    act(("idb", ALL), ("idf", ALL), ACT.Copy)
    act(("big", ALL), ("idf", ALL), ACT.Copy, 2.0 ** 23)
    act(("hf", ALL), ("idf", ALL), ACT.Copy, -0.5)

    def hand_on(t, h):
        n, pay, co = K * CH, "pay%d" % h, "co%d" % h
        if cfg["co"] == "M":
            send([((pay, t, 0, sl(0, 4)), (pay, t, 1, sl(0, 4))), ((pay, t, 0, sl(4, 4)), (pay, t, 1, sl(4, 4))), ((co, t, 0), (co, t, 1))], 12 * n)
        else:
            send([((pay, t, 0), (pay, t, 1))], 8 * n)
        tag[0] = "v%d%d" % (t, h)
        if cfg["co"] == "V":
            cp((co, t, 1), offsets(t, h, 1))
        mm("x%d%da" % (t, h), [(cols("xp", h * 256, n), ("idf", ALL), (co, t, 0))], True)
        mm("x%d%db" % (t, h), [(cols("xp", h * 256 + n, n - CH), ("idf", ALL), (co, t, 0, slice(0, n - CH)))], True)
        for r in range(K):
            tt(("eq%d" % h, r), (co, t, 1), cols("xp", h * 256 + r * CH, n), ALU.is_equal)
        tag[0] = "i"

    def offsets(t, h, li, first=0, n=K):
        return cols("off%d" % h, (t * 16 + li * K + first) * CH, n * CH)

    ts(("tb", ALL), ("ndl", ALL), 7, None, ALU.bitwise_and)
    ts(("tj", ALL), ("ndl", ALL), 3, None, ALU.arith_shift_right)
    for h in range(H):
        half, tmp = (ALL, sl(h * CH, CH)), ("sp", 2 * h + 1, slice(4, 8), ALL)
        ts(tmp, ("tb",) + half, float(L), None, ALU.mult)
        tt(("tq",) + half, ("tj",) + half, tmp, ALU.add)
        cp(offsets(0, h, 0), ("tq",) + half)
        send([(offsets(0, h, 0), offsets(0, h, 1))], 2 * K * CH)
        marks["m%d" % h] = len(ops) - 1
        ts(("pay%d" % h, 0, 0, ALL, slice(0, CH)), ("tq",) + half, 6, None, ALU.arith_shift_right)
        ts(("pay%d" % h, 0, 0, ALL, slice(CH, 2 * CH)), ("tq",) + half, 63, None, ALU.bitwise_and)
        cp(("co%d" % h, 0, 0), ("tq",) + half)
        hand_on(0, h)
    for b in range(8):
        move(cfg["prel"][b], cols("pw0", b * L, L), ("praw", ALL, (b + 1) % 8))

    def loads(mark):
        gate, keep = marks.get(mark), tag[0]
        tag[0] = "l" + mark
        for what in [w for w in sorted(cfg["gates"]) if cfg["gates"][w] == mark]:
            if what == "e":
                dma("Y", ("eraw", ALL), ("ea", ALL), 6144, gate=gate)
                dma("Y", ("dls", ALL), ("dl", ALL), 4, gate=gate)
                for j in range(2):
                    act(cols("mc", j, 1), ("dls", ALL), ACT.Copy, 4.0 * j - 2.0)
                for b in range(8):
                    move(cfg["erel"][b], cols("ew", b * L, L), ("eraw", ALL, (b + 1) % 8))
            elif what == "p":
                dma("Y", cols("pw1", 0, 6 * L), cols("pw0", L, 6 * L), 12 * L, gate=gate)
                dma("Y", cols("pw1", 7 * L, L), cols("pw0", 0, L), 2 * L, gate=gate)
                dma("Y", cols("pw1", 6 * L, L), cols("fc", 0, L), 2 * L, gate=gate)
            elif what == "x":
                dma("Y", ("xr", ALL), ("er", ALL), 3072, gate=gate)
                dma("Y", cols("ew", 8 * L, 3 * L), cols("ew", 0, 3 * L), 12 * L, gate=gate)
                for t in (2, 3):
                    dma("Y", cols("pw%d" % (t % 2), 9 * L, L), cols("pw0", (t - 1) * L, L), 2 * L, gate=gate)
                    dma("Y", cols("pw%d" % (t % 2), 8 * L, L), cols("fc", (t - 1) * L, L), 2 * L, gate=gate)
            else:
                rows, n2 = sl(int(what) * H, H), LH
                dma("Y", ("fr", rows, sl(0, LH)), cols("fc", int(what) * L, L), 2 * L, gate=gate)
                while n2 < max(cfg["nc"]) * LH:
                    dma("Y", ("fr", rows, sl(n2, n2)), ("fr", rows, sl(0, n2)), 2 * H * n2)
                    n2 *= 2
        tag[0] = keep

    for m in ("", "m0", "m1"):
        loads(m)

    def choice(t, h):
        kp, dd, rr, pay, co, sfx = "kp%d" % h, "dd%d" % h, "rr%d" % h, "pay%d" % h, "co%d" % h, "%d%d" % (t, h)
        win = cols("pw%d" % (t % 2), (t - t % 2) * L, W)
        folded = any(c in "sv" for s in cfg["slots"][t][h] for c in s)

        def wires(mem, pos, li):
            s = sl(pos[0], len(pos), pos[1] - pos[0] if len(pos) > 1 else 1)
            if mem == "F":
                return ("fin%d" % h, s, ALL)
            if mem == "S":
                return ("ss%d" % h, li, s, ALL)
            return ("sp", slice(2 * h, 2 * h + 2) if li is ALL else 2 * h + li, s, ALL)

        def cx(big, o, a, b):
            tt(wires(*o), wires(*a), wires(*b), ALU.max if big else ALU.min)

        def pas(w, src, s0, ns):
            ko = (kp, s0 // K, sl(s0 % K, ns), slice(0, CH))
            for r0 in range(0, 16, cfg["run"]):
                mm("k" + sfx, [(ko, cols(w, 15 - r, 128), src[:-1] + (sl(src[-1].start + r, ns * CH, 16),)) for r in range(r0, r0 + cfg["run"])])

        tag[0] = "o" + sfx
        mm("k" + sfx, [((kp, ALL, ALL, slice(0, CH)), ("idb", ALL), ("t2", ALL))], True)
        for li in range(2):
            tag[0] = "oa"[li] + sfx
            how = cfg["slots"][t][h][li]
            for kind, a0, n0 in runs([{"s": "f", "v": "f", "B": "S", "A": "V"}.get(c, c) for c in how]):
                step = cfg["fold"] // 2 if kind == "f" else cfg["nc"][li] // 2 if t else 2
                for a in range(a0, a0 + n0, step):
                    n = min(step, a0 + n0 - a)
                    s0, ns = li * K + 2 * a, 2 * n
                    d_, r_ = cols(dd, s0 * LH, ns * LH), cols(rr, s0 * LH, ns * LH)
                    if kind == "f":
                        for e, b, m in runs(how[a:a + n]):
                            gather(e.upper(), cols(dd, (s0 + 2 * b) * LH, 2 * m * LH), win, offsets(t, h, li, 2 * (a + b), 2 * m))
                        w = 4 if ns % 4 == 0 else 2
                        fold([((cols(dd, s * LH, w * LH), ("fr", t * H + h, slice(0, w * LH))), cols(rr, s * LH, w * LH))
                              for s in range(s0, s0 + ns, w)], r_, 2, 2 * ns * LH)
                        pas("wn", d_, s0, ns)
                        pas("w2", r_, s0, ns)
                        continue
                    ff = ("fr", t * H + h, slice(0, ns * LH))
                    if kind == "V":
                        gather("V", d_, win, offsets(t, h, li, 2 * a, ns), minus=ff)
                    else:
                        gather("S", d_, win, offsets(t, h, li, 2 * a, ns), -1.0)
                        dma("G", d_, ff, 2 * ns * LH, True)
                    if folded:
                        pas("w1", ff, s0, ns)
                    for c, b, m in runs(how[a:a + n]):
                        d_, r_ = cols(dd, (s0 + 2 * b) * LH, 2 * m * LH), cols(rr, (s0 + 2 * b) * LH, 2 * m * LH)
                        if c in "AB":
                            act(r_, d_, ACT.Abs)
                        else:
                            ts(r_, d_, 0.0, -2.0, ALU.min, ALU.mult)
            for buf, kinds in ((dd, "SV"), (rr, "SVAB")):
                for use, a, n in runs([c in kinds for c in how]):
                    if use:
                        pas("w1", cols(buf, (li * K + 2 * a) * LH, 2 * n * LH), li * K + 2 * a, 2 * n)
        for r0 in (0, 4):
            mm("k" + sfx, [((kp, 1, ALL, slice(0, CH)), ("big", ALL), ("eq%d" % h, r)) for r in range(r0, r0 + 4)])
        if h == H - 1 and t < R - 2:
            dma("Y", cols(win[0], 7 * L, L), cols("fc", t * L, L), 2 * L)
        tag[0] = "s" + sfx
        for q in (0, 1):
            for ab in (0, 1):
                o = wires("SP"[q], [0, 1, 2, 3], ALL)
                tt(o[:3] + (sl(ab * CH, CH),), (kp, ALL, sl(4 * q, 4), slice(0, CH)), (pay, t, ALL, sl(4 * q, 4), sl(ab * CH, CH)), ALU.add)
        marks["k" + sfx] = len(ops) - 1
        loads("k" + sfx)
        for big, o, a, b in NET8:
            cx(big, o + (ALL,), ("S", a, ALL), ("P", b, ALL))
        marks["n" + sfx] = len(ops) - 1
        loads("n" + sfx)
        for c in MERGE:
            cx(*c)
        tmp = ("sp", 2 * h + 1, slice(4, 8), ALL)
        ts((pay, t + 1, 0), ("fin%d" % h, ALL), 63, None, ALU.bitwise_and)
        ts(tmp, (pay, t + 1, 0, ALL, slice(0, CH)), 64.0, None, ALU.mult)
        tt((co, t + 1, 0), (pay, t + 1, 0, ALL, slice(CH, 2 * CH)), tmp, ALU.add)
        cp(offsets(t + 1, h, 0), (co, t + 1, 0))
        if t < R - 1:
            send([(offsets(t + 1, h, 0), offsets(t + 1, h, 1))], 2 * K * CH)
            hand_on(t + 1, h)

    def errors(t):
        ga, bs, last = "ga%d" % t, "bs%d" % t, t == R - 1
        for q in range(4):
            h, a = q // 2, q % 2 * 4
            tag[0] = "g%d%d" % (t, h)
            how = cfg["egather"][t][q]
            for eng, a0, n0 in ([(how.upper(), a, 4)] if how != "x" else [("V", a, 2), ("S", a + 2, 2)]):
                gather(eng, (ga, h, sl(a0 * LH, n0 * LH)), cols("ew", t * L, W), offsets(t + 1, h, 0, a0, n0), -1.0)
        parts = [(h, j * LH // len(s), LH // len(s), int(c)) for h, s in enumerate(cfg["chain"][t].split()) for j, c in enumerate(s)]

        def bank(p, k=K):
            h, a, n, _ = parts[p]
            if last:
                return cols(("bp0", "bp1", "bp2", "xp")[2 * h + (k % 2 if n == LH else a // n)], 0, n)
            return cols("bp%d" % ((2 * k + p) % 3), 0, n)

        def gk(k, p, buf=ga):
            return (buf, parts[p][0], sl(k * LH + parts[p][1], parts[p][2]))
        lim = (cols("mc", 1, 1), cols("mc", 0, 1), ALU.min, ALU.max)
        for k in range(K + 1):
            for p, (h, a, n, skip) in enumerate(parts):
                tag[0] = "e%d%d" % (t, h)
                lanes, apart = sl(h * LH + a, n), K - skip
                u, s_, grp = bank(p, k), ("uu", 0, lanes), "u%d%d%d" % (t, p, k)
                terms = ([gk(k, p)] if k < K else []) + [s_] + [("uu", 1 + j - apart, lanes) for j in range(apart, k)]
                if k == 0:
                    ts(s_, gk(0, p), *lim)
                    continue
                for j, term in enumerate(terms):
                    mm(grp, [(u, ("hf" if j or k == K else "idf", ALL), term)], j == 0)
                if k < apart:
                    ts(u, u, *lim)
                    tt(s_, s_, u, ALU.add)
                elif k < K:
                    ts(("uu", 1 + k - apart, lanes), u, *lim)
                elif not last:
                    tt(cols("ew", (7 + t) * L + h * LH + a, n), cols("xr", t * L + h * LH + a, n), u, ALU.subtract)
        if last:
            for h in range(H):
                tag[0] = "q%d" % h
                sm, ng = ("kp%d" % h, 0, slice(0, 6), ALL), ("sp", 2 * h, slice(0, 8), ALL)
                mine = [p for p in range(len(parts)) if parts[p][0] == h]
                for j in range(2 if cfg["qadd"][h] == "D" else 1):
                    for p in mine:
                        act(gk(j, p, bs), bank(p), ACT.Copy)
                dma("Y", cols("yb", t * L + h * LH, LH), (bs, h, slice(0, LH)), 768)
                for k in range(K):
                    if cfg["qadd"][h] == "V":
                        for p in mine:
                            tt(gk(k, p), gk(k, p), bank(p), ALU.add)
                    elif k % 2 == 0:
                        dma("G", (ga, h, sl(k * LH, 2 * LH)), (bs, h, slice(0, 2 * LH)), 1536, True)
                for k in range(0, K, 2):
                    g_ = (ga, h, sl(k * LH, 2 * LH))
                    if k >= K - cfg["vabs"][h]:
                        for j in (k, k + 1):
                            gj = (ga, h, sl(j * LH, LH))
                            ts(ng, gj, -1.0, None, ALU.mult)
                            tt(gj, gj, ng, ALU.max)
                    else:
                        act(g_, g_, ACT.Abs)
                    act(g_, g_, ACT.Exp, -1.0)
                    for j in range(k, min(k + 2, K - 1)):
                        mm("q%d" % h, [(sm, ("idf", ALL), (ga, h, sl(j * LH, LH)))], j == 0)
                tt(("so", t, sl(h * LH, LH)), (ga, h, sl((K - 1) * LH, LH)), sm, ALU.add)
                dma("Y", cols("ys", t * L + h * LH, LH), ("so", t, sl(h * LH, LH)), 768)
            return
        tag[0] = "b%d" % t
        for p in range(len(parts)):
            for j in range({"D": 1, "F": 1, "E": 2, "C": 4}[cfg["padd"][t]]):
                act(gk(j, p, bs), bank(p), ACT.Copy)

    def spread(t):
        ga, bs = "ga%d" % t, "bs%d" % t
        tag[0] = "p%d" % t
        copies = {"D": 1, "F": 1, "E": 2, "C": 4}[cfg["padd"][t]]
        b_ = (bs, ALL, slice(0, LH))
        dma("Y", cols("yb", t * L, L), b_, 1536)
        if cfg["padd"][t] != "F":
            while copies < cfg["bc"]:
                dma("Y", (bs, ALL, sl(copies * LH, copies * LH)), (bs, ALL, sl(0, copies * LH)), 1536 * copies)
                copies *= 2
            if copies == 4:
                for q in range(2):
                    for h in range(H):
                        dma("G", (ga, h, sl(q * 4 * LH, 4 * LH)), (bs, h), 3072, True)
            else:
                for q in range(4):
                    dma("G", (ga, ALL, sl(q * 2 * LH, 2 * LH)), (bs, ALL, sl(0, 2 * LH)), 3072, True)
        else:
            for h in range(H):
                fold([(((ga, h, sl(k * LH, LH)), (bs, h, slice(0, LH))), (ga, h, sl(k * LH, LH))) for k in range(K)], (ga, h), 1, 4 * K * LH)
        for q in range(4):
            g_ = (ga, ALL, sl(q * 2 * LH, 2 * LH))
            if t == R - 2 and q >= 4 - cfg["pabs"]:
                for h in range(H):
                    gh, ng = (ga, h, sl(q * 2 * LH, 2 * LH)), ("sp", slice(2, 4), slice(0, 8), ALL)
                    ts(ng, gh, -1.0, None, ALU.mult)
                    tt(gh, gh, ng, ALU.max)
            else:
                act(g_, g_, ACT.Abs)
            act(g_, g_, ACT.Exp, -1.0)
            if cfg["psum"][t] == "V" and q in (1, 2):
                dma("G", (ga, ALL, sl(0, 2 * LH)), g_, 3072, True)
        if cfg["psum"][t] == "V":
            acc = ("sp", slice(1, 4, 2), slice(0, 8), ALL)
            tt(acc, (ga, ALL, sl(6 * LH, LH)), (ga, ALL, sl(7 * LH, LH)), ALU.add)
            tt(acc, (ga, ALL, sl(LH, LH)), acc, ALU.add)
            tt(("so", t), (ga, ALL, sl(0, LH)), acc, ALU.add)
            dma("Y", cols("ys", t * L, L), ("so", t), 1536)
        elif cfg["psum"][t] == "D":
            for n2 in (4 * LH, 2 * LH, LH):
                dma("G", (ga, ALL, sl(0, n2)), (ga, ALL, sl(n2, n2)), 4 * n2 * H, True)
            dma("Y", cols("ys", t * L, L), (ga, ALL, sl(0, LH)), 1536)
        elif cfg["psum"][t] == "P":
            sm = ("kp0", ALL, slice(0, 6), ALL)
            mm("p", [(sm, ("idf", ALL), (ga, ALL, sl(0, LH)))], True)
            for k in range(1, K):
                for h in range(H):
                    mm("p", [(("kp0", h, slice(0, 6), ALL), ("idf", ALL), (ga, h, sl(k * LH, LH)))])
            act(("so", t), sm, ACT.Copy)
            dma("Y", cols("ys", t * L, L), ("so", t), 1536)
        else:
            fold([([(ga, h, sl(k * LH, LH)) for k in range(K)], ("so", t, sl(h * LH, LH))) for h in range(H)], ("so", t), 1, 4 * L)
            dma("Y", cols("ys", t * L, L), ("so", t), 1536)

    for t in range(R):
        for h in range(H):
            choice(t, h)
        for t2 in range(t):
            if t == (t2 + 1 if cfg["psum"][t2] in "DF" else R - 1):
                spread(t2)
        errors(t)
    return ops


def analyse(cfg):
    ops = build_ops(cfg)
    SC = scratch(cfg)
    index = {b: np.arange(int(np.prod(v[1][1:]))).reshape(v[1][1:]) for b, v in SC.items()}
    lastw = {b: np.full(index[b].size, -1) for b in SC}
    readers = {b: [] for b in SC}
    adders = {b: [] for b in SC}
    bank = {}
    deps, fed = [], []

    def mask(a):
        m = np.zeros(index[a[0]].size, bool)
        m[index[a[0]][a[1:]].ravel()] = True
        return m

    def meet(users, m):
        return [j for j, mj in users if np.any(mj & m)]

    for i, o in enumerate(ops):
        raw = set([o["after"]] if "after" in o else [])
        d = set()
        for a in o["rd"]:
            m = mask(a)
            raw.update(int(v) for v in np.unique(lastw[a[0]][m]))
            raw.update(meet(adders[a[0]], m))
        for a in o["acc"] + o["wr"]:
            m = mask(a)
            d.update(int(v) for v in np.unique(lastw[a[0]][m]))
            d.update(meet(readers[a[0]], m))
        for a in o["wr"]:
            m = mask(a)
            d.update(meet(adders[a[0]], m))
            for users in (readers, adders):
                users[a[0]] = [(j, mj & ~m) for j, mj in users[a[0]] if np.any(mj & ~m)]
        touched = set()
        for a in o["rd"] + o["wr"] + o["acc"]:
            if SC[a[0]][0] == "psum":
                touched.update((a[0], int(v)) for v in np.unique(index[a[0]][a[1:]] // 512))
        for b in touched:
            eng, js, before = bank.get(b, (o["eng"], [], []))
            if eng != o["eng"]:
                js, before = [], js
            d.update(before)
            bank[b] = (o["eng"], js + [i], before)
        for a in o["rd"] if o["kind"] != "fold" else []:
            readers[a[0]].append((i, mask(a)))
        for a in o["acc"]:
            adders[a[0]].append((i, mask(a)))
        for a in o["wr"]:
            lastw[a[0]][index[a[0]][a[1:]].ravel()] = i
        d = (d | raw) - {-1, i}
        known = 0
        for j in d:
            known |= fed[j]
        d = {j for j in d if not known >> j & 1 or j == o.get("after")}
        for j in d:
            known |= 1 << j
        deps.append(sorted((d | {o.get("behind")}) - {None}))
        fed.append(0 if o["kind"] == "recv" and ops[o["after"]]["kind"] == "send" else known)
    return ops, deps, fed


def times(ops, c):
    out = []
    for o in ops:
        e, k, n = o["eng"], o["kind"], o["work"]
        if k == "g":
            out.append(((50 if e == "V" else 65) + c["cy"] * c["ga"] * n, 0.0, 0.0))
        elif k == "c":
            fix = {"V": c["ov"], "S": 65.0, "P": 0.0, "G": 170.0}[e]
            out.append((fix + c["cy"] * max(n, c["mn"] if e == "V" else 0), 0.0, 60.0 if e == "P" else 0.0))
        elif k == "dma":
            out.append((c["dg"] if e == "G" else 80.0, n / c["db"] + o["rows"] * c["row"], c["dl"]))
        elif k == "send":
            far = (64 if len(o["pairs"]) > 2 else 16 * len(o["pairs"])) * c["far"]
            out.append((c["rg"], n / c["db"] + far / 2, c["rl"] + n / c["rb"] + far / 2))
        elif k == "fold":
            out.append((c["rg"], len(o["pairs"][0][0]) * n / c["db"], c["fl"] + n / c["fb"]))
        else:
            out.append((0.0, 0.0, 0.0))
    return out


def graph(ops, before, after, soft, c, back=False):
    tm = times(ops, c)
    eng = [o["eng"] for o in ops]
    edges = []
    for i in range(len(ops)):
        row = []
        for j in after[i]:
            if eng[i] == eng[j] and ((i, j) in soft or (j, i) in soft):
                v = -sum(tm[j][1:]) if back else -sum(tm[i][1:])
            elif eng[i] is None or eng[j] is None:
                v = c["hop"] if (eng[i] is None) != back else 0.0
            else:
                v = c["same"] if eng[i] == eng[j] else c["hop"]
            row.append((j, v + (tm[j][1] + tm[j][2] if back else 0.0)))
        edges.append(row)
    if back:
        return [(t[0], 0.0, 0.0) for t in tm], eng, edges, [len(d) for d in before], [t[1] + t[2] for t in tm]
    return tm, eng, edges, [len(d) for d in before], [0.0] * len(ops)


def run(gr, prio=None, order=None, look={}):
    tm, eng, edges, left, ready = gr
    n = len(eng)
    left, ready = list(left), list(ready)
    done, start = [0.0] * n, [0.0] * n
    free = {e: 0.0 for e in "VSPGY"}
    out = {e: [] for e in "VSPGY"}
    pool = {e: [i for i in range(n) if eng[i] == e and not left[i]] for e in "VSPGY"}
    head = {e: order[e][0] for e in order} if order else None
    dmas = 0.0
    while True:
        t0, e = 1e30, None
        for q in "VSPGY":
            if order:
                i = head[q]
                if i is None or left[i]:
                    continue
                v = ready[i]
            elif pool[q]:
                v = min([ready[j] for j in pool[q]])
            else:
                continue
            if v < free[q]:
                v = free[q]
            if v < t0:
                t0, e = v, q
        if e is None:
            return out, start, done
        if order:
            i = head[e]
            p = len(out[e]) + 1
            head[e] = order[e][p] if p < len(order[e]) else None
        else:
            t1 = t0 + look.get(e, 0.0)
            i = -max([(prio[j], -j) for j in pool[e] if ready[j] <= t1])[1]
            pool[e].remove(i)
            t0 = max(t0, ready[i])
        start[i] = t0
        t = free[e] = t0 + tm[i][0]
        out[e].append(i)
        if tm[i][1]:
            t = dmas = max(dmas, t) + tm[i][1]
        todo = [(i, t + tm[i][2])]
        while todo:
            i, t = todo.pop()
            done[i] = t
            for j, v in edges[i]:
                if t + v > ready[j]:
                    ready[j] = t + v
                left[j] -= 1
                if not left[j]:
                    if eng[j] is None:
                        todo.append((j, ready[j]))
                    elif not order:
                        pool[eng[j]].append(j)


def plan_order(cfg, known, costs, judges):
    ops, deps, fed = known
    n = len(ops)
    succ = [[] for _ in range(n)]
    soft = set()
    for i in range(n):
        for j in deps[i]:
            succ[j].append(i)
            if ops[i]["eng"] == ops[j]["eng"] == "P" or ops[i].get("behind") == j:
                soft.add((j, i))
    ahead, back = graph(ops, deps, succ, soft, costs), graph(ops, succ, deps, soft, costs, True)
    views = [(graph(ops, deps, succ, soft, c), c["cy"]) for c in judges]

    def judge(order):
        return sum(max(run(g, order=order)[2]) / cy for g, cy in views)
    tm = times(ops, costs)
    path = [0.0] * n
    for i in range(n - 1, -1, -1):
        path[i] = sum(tm[i]) + max([path[j] + costs["same"] for j in succ[i]] + [0.0])
    kinds = sorted(set(o["tag"] + str(o["eng"]) for o in ops))
    kind = [kinds.index(o["tag"] + str(o["eng"])) for o in ops]
    rs = np.random.RandomState(cfg.get("seed", 0))
    kind = np.array(kind)
    order, _, done = run(ahead, prio=path)
    best = (judge(order), order, done, np.array(path))
    for turn in range(cfg["tries"]):
        if turn < 3 or turn % 40 == 0:
            prio = np.array(run(back, prio=done if turn < 3 else best[2])[2])
        else:
            prio = best[3] + ((rs.rand(len(kinds)) < cfg["share"]) * rs.randn(len(kinds)) * cfg["move"])[kind]
        order, _, done = run(ahead, prio=prio.tolist(), look=cfg["look"])
        v = judge(order)
        if v <= best[0]:
            best = (v, order, done, prio)
    return best[1], soft, succ


def make_plan(cfg):
    known = analyse(cfg)
    ops, deps, _ = known
    order, soft, _ = plan_order(cfg, known, COSTS, JUDGES)
    pos = {}
    for e in order:
        for p, i in enumerate(order[e]):
            pos[i] = p
    needed = set()
    waits = {}
    for e in order:
        seen = {}
        for i in order[e]:
            w = {}
            for j in deps[i]:
                if (j, i) in soft:
                    continue
                key, val = (ops[j]["eng"], pos[j]) if ops[j]["kind"] in "cg" else (j, 0)
                if seen.get(key, -1) < val:
                    w[key] = max(w.get(key, -1), val)
            seen.update(w)
            waits[i] = w
            for key, val in w.items():
                needed.add(order[key][val] if key in order else key)
    count = {}
    for e in order:
        c = 0
        for i in order[e]:
            if ops[i]["kind"] in "cg" and i in needed:
                c += 1
                count[i] = c
    sems = {}
    for i, o in enumerate(ops):
        if o["kind"] in ("dma", "recv"):
            sems[i] = "d%d" % len(sems)
    closes = {ops[i]["group"]: i for i in order["P"]}
    return {"ops": ops, "order": order, "waits": waits, "needed": needed, "count": count, "sems": sems, "closes": set(closes.values())}


def helpers(T, topo):
    out = {}
    for c in T.cores:
        out[c] = [k for k in topo.cores_of(c) if T.rank_of(k) is None and topo.die(k) == topo.die(c) and k not in out.values()][0]
    return out


def shares(engines, n):
    size = [len(engines)]
    while len(size) < n:
        size.sort()
        size = size[:-1] + [size[-1] // 2] * 2
    size.sort(reverse=True)
    return [sum(1 << e for e in engines[sum(size[:j]):sum(size[:j + 1])]) for j in range(n)]


def rank_program(g, core, T, topo):
    if "p" not in PLAN:
        PLAN["p"] = make_plan(CFG)
    p = PLAN["p"]
    ops, order, sems = p["ops"], p["order"], p["sems"]
    helper = helpers(T, topo)
    recv_of = {o["after"]: j for j, o in enumerate(ops) if o["kind"] == "recv"}

    def ap(a):
        return T[a[0]][(ALL,) + a[1:]]

    rank = T.rank_of(core)
    if rank is None:
        for home in [c for c in helper if helper[c] == core]:
            rid, pid, _ = topo.addr(home)
            n, sent = len(topo.engines(core, home)), 0
            for i in order["G"]:
                if ops[i]["kind"] == "fold":
                    s = T.sem[sems[recv_of[i]]]
                    g.wait_ge(s, n)
                    g.remote_dma(ap(ops[i]["back"]), ap(ops[i]["back"]), s, T.sem.out, pid, rid, topo.mask(core, home))
                    sent += n
            if sent:
                g.wait_ge(T.sem.out, sent)
        return
    nxt = T.cores[(rank + 1) % len(T.cores)]
    assert topo.may_write(core, nxt)
    ne = min(len(topo.engines(a, b)) for a, b in zip(T.cores, T.cores[1:] + T.cores[:1]))
    way = {"send": (nxt, topo.engines(core, nxt)[:ne]), "fold": (helper[core], topo.engines(core, helper[core]))}
    x = {"V": g.vector, "S": g.scalar, "P": g.tensor, "G": g, "Y": g.sync, "ap": ap}
    for e in "YGVSP":
        q = x[e]
        late, sent = [], 0
        for i in order[e]:
            o = ops[i]
            for key, val in p["waits"][i].items():
                if key in order:
                    q.wait_ge(T.sem["c" + key], p["count"][order[key][val]])
                else:
                    q.wait_ge(T.sem[sems[key]], len(way[ops[ops[key]["after"]]["kind"]][1]) if ops[key]["kind"] == "recv" else 16)
            if o["kind"] in way:
                dst, engines = way[o["kind"]]
                rid, pid, _ = topo.addr(dst)
                masks = shares(engines, len(o["pairs"]))
                s = T.sem[sems[recv_of[i]]]
                if o["kind"] == "fold":
                    g.remote_dma_fused([RemoteDMATransfer(dst_ids=[DstId(rid=rid, pnc=pid)], dma_engine_mask=m, remote_sem=s,
                                                          srcs=[ap(a) for a in srcs], dsts=[ap(d)], alu_op=o["alu"])
                                        for (srcs, d), m in zip(o["pairs"], masks)], local_sem=T.sem.out)
                elif len(masks) > 1:
                    g.remote_dma_fused([RemoteDMATransfer(dst_ids=[DstId(rid=rid, pnc=pid)], dma_engine_mask=m, remote_sem=s,
                                                          src=ap(a), dst=ap(d)) for (a, d), m in zip(o["pairs"], masks)], local_sem=T.sem.out)
                else:
                    g.remote_dma(ap(o["pairs"][0][1]), ap(o["pairs"][0][0]), s, T.sem.out, pid, rid, masks[0])
                sent += len(engines)
            elif o["kind"] == "dma":
                o["emit"](x).then_inc(T.sem[sems[i]], 16)
                if i not in p["needed"]:
                    late.append(sems[i])
            else:
                x["stop"] = i in p["closes"]
                ins = o["emit"](x)
                if i in p["needed"]:
                    ins.then_inc(T.sem["c" + e], 1)
        for s in late:
            q.wait_ge(T.sem[s], 16)
        if sent:
            q.wait_ge(T.sem.out, sent)
